import numpy as np, ml_dtypes
CORES = [24,25,26,27,28,29,30,31]
N = 8
BF = ml_dtypes.bfloat16
def gentries(a):
    return np.ascontiguousarray(a.reshape(8, 16, -1).transpose(0, 2, 1)).reshape(8, -1)
def gtable(e):
    e = np.asarray(e); return np.ascontiguousarray(e.reshape(8, -1, 16).transpose(0, 2, 1)).reshape(128, -1).astype(np.int32)
L, XW, YW, R, SL = 1, 128, 64, 512, 48
C = XW * YW
SLR = np.arange(128) % 16 >= 14
def pack(e, fc, x, v, u, w):
    g = lambda a: np.stack([gtable(t) for t in a])
    return {"lay": e.astype(np.float32).astype(BF), "fac": np.repeat(fc, 16, axis=1).astype(np.int32), "px": g(x), "py": g(v), "dx": g(u), "dy": g(w)}
def parts(rng):
    e = rng.integers(-120, 121, (N, 128, L * C), dtype=np.int16)
    e[:, SLR] = rng.integers(-SL, SL + 1, (N, 16, L * C), dtype=np.int16)
    fc = np.stack([np.stack([rng.permutation(16)[:8] + 1 for l in range(L)], axis=1) for r in range(N)])
    return [e, fc, rng.integers(0, 16 * XW, (N, 8, R)), rng.integers(0, 16 * YW, (N, 8, R)), rng.integers(-16, 17, (N, 8, R)), rng.integers(-16, 17, (N, 8, R))]
def setup_inputs(rng):
    return pack(*parts(rng))
def setup_inputs_prism(rng):
    e, fc, x, v, u, w = parts(rng)
    return pack(np.tile(e[:, :16], (1, 8, 1)), fc, *[np.repeat(a[:, :1], 8, axis=1) for a in (x, v, u, w)])
def setup_inputs_steep(rng):
    e, fc, x, v, u, w = parts(rng); g = int(rng.integers(0, 8))
    e[:, SLR] = SL * rng.choice(np.array([-1, 1]), (N, 16, L * C)); fc[:] = 16
    u = 16 * rng.choice(np.array([-1, 1]), u.shape); w = 16 * rng.choice(np.array([-1, 1]), w.shape)
    e[:, 16 * g] = 120; e[:, 16 * g + 1] = -120; e[:, 16 * g + 14] = SL; e[:, 16 * g + 15] = -SL; u[:, g] = 16; w[:, g] = -16
    return pack(e, fc, x, v, u, w)
def setup_inputs_edges(rng):
    e, fc, x, v, u, w = parts(rng)
    e[:, SLR] = rng.choice(np.array([-8, -1, 0, 1, 8]), (N, 16, L * C)); fc = rng.choice(np.array([1, 2, 15, 16]), fc.shape)
    x = rng.choice(np.array([0, 15, 16, 16 * XW - 16, 16 * XW - 1]), x.shape); v = rng.choice(np.array([0, 15, 16, 16 * YW - 16, 16 * YW - 1]), v.shape)
    u = rng.choice(np.array([-16, -1, 0, 1, 16]), u.shape); w = rng.choice(np.array([-16, -1, 0, 1, 16]), w.shape)
    return pack(e, fc, x, v, u, w)
def setup_inputs_one(rng):
    p = parts(rng); q = int(rng.integers(0, N))
    for i in range(2, 6):
        p[i] = np.repeat(p[i][:, :, :16], R // 16, axis=2); p[i][q] = p[i][q][:, :1]
    return pack(*p)
def setup_inputs_spread(rng):
    e, fc, x, v, u, w = parts(rng)
    z = rng.random(e.shape, dtype=np.float32); e[z < 0.5] = 0; k = z > 0.9; b = np.where(SLR, SL, 120)[None, :, None]
    e = np.where(k, np.where(e < 0, -b, b), e)
    x = np.floor(rng.random(x.shape) ** 4 * (16 * XW)).astype(np.int64); v = np.floor(rng.random(v.shape) ** 4 * (16 * YW)).astype(np.int64)
    return pack(e, fc, x, v, u, w)
def check_inputs(d):
    bad = []; e = d["lay"].astype(np.float32); fc = d["fac"]
    if not np.array_equal(e, np.floor(e)): bad.append("whole numbers in lay")
    if not np.abs(e[:, ~SLR]).max() <= 120: bad.append("emission")
    if not np.abs(e[:, SLR]).max() <= SL: bad.append("slopes")
    if not (fc.min() >= 1 and fc.max() <= 16): bad.append("factors")
    if not np.array_equal(fc, np.repeat(fc[:, ::16], 16, axis=1)): bad.append("factors alike in a group")
    if not (d["px"].min() >= 0 and d["px"].max() < 16 * XW and d["py"].min() >= 0 and d["py"].max() < 16 * YW): bad.append("places")
    if not (min(d["dx"].min(), d["dy"].min()) >= -16 and max(d["dx"].max(), d["dy"].max()) <= 16): bad.append("directions")
    return bad
def reference(lay, fac, px, py, dx, dy):
    t = lay.astype(np.float32).astype(np.int32).reshape(N, 8, 16, L, C)
    y = np.zeros((N, 128, R), np.float32); g8 = np.arange(8)[:, None, None]; c16 = np.arange(16)[None, :, None]
    for r in range(N):
        x, v, u, w = [gentries(a[r]).astype(np.int64) for a in (px, py, dx, dy)]
        s = np.zeros((8, 16, R), np.int64)
        for h in range(N):
            q = (r + h) % N
            for l in range(L):
                fc = fac[q, ::16, l].astype(np.int64)[:, None]
                cell = (v >> 4) * XW + (x >> 4)
                p = t[q][g8, c16, l, cell[:, None, :]].astype(np.int64)
                s = s + p
                u = u + ((fc * p[:, 14]) >> 7); w = w + ((fc * p[:, 15]) >> 7)
                x = (x + u) & (16 * XW - 1); v = (v + w) & (16 * YW - 1)
        y[r] = s.reshape(128, R).astype(np.float32)
    return {"y": y}

@@ -1,0 +1,350 @@
+from concourse.bass import DstId, RemoteDMATransfer
+from concourse.mybir import AluOpType, ActivationFunctionType
+
+N = 8
+C = 8192
+O = [0, 1, 1, 1, 4, 4, 4]
+WIN = {0: (0, 0, None), 1: (1, 0, None), 2: (0, 2, 1)}
+IMPORTS = [1, 2]
+ACT_E = {4: [1], 5: [2], 6: [3, 4, 5]}
+DVE_E = {6: [0, 6]}
+G_ORDER = "st0 sl2 id st3 ix2+ix3 ix5 G1 ix6 G2 ix7 G3 G4 G5 G6 G7".split()
+SYNC_ORDER = [("lay", 1), ("done", 0), ("lay", 1), ("win", 1), ("lay", 1), ("win", 2), ("lay", 3), ("done", 3), ("lay", 2)]
+PE_ORDER = [1, 2, 0, 3, 4, 5, 6]
+IDENT_AFTER = 3
+SPLIT = 14
+BIAS = 1536.0
+RB = BIAS - 127.0 / 32.0
+
+SCRATCH = {
+    "ly": ("sbuf", [128, C], "bfloat16"),
+    "w0": ("sbuf", [128, C], "bfloat16"),
+    "w1": ("sbuf", [128, C], "bfloat16"),
+    "stage": ("dram", [128, 1024], "bfloat16"),
+    "land": ("dram", [7, 128, 1024], "bfloat16"),
+    "fown": ("sbuf", [128, 1], "int32"),
+    "fl": ("sbuf", [128, 8], "int32"),
+    "fs0": ("sbuf", [128, 1], "float32"),
+    "fs": ("sbuf", [128, 8], "float32"),
+    "raw": ("sbuf", [128, 128], "int32"),
+    "hist": ("sbuf", [128, 64 * 24], "int32"),
+    "pre": ("sbuf", [128, 64], "float32"),
+    "tw": ("sbuf", [128, 64], "float32"),
+    "cx": ("sbuf", [128, 32], "int32"),
+    "cy": ("sbuf", [128, 32], "int32"),
+    "cell": ("sbuf", [128, 32], "int32"),
+    "ixl": ("sbuf", [128, 32 * 8], "uint16"),
+    "ixr": ("sbuf", [128, 32 * 8], "uint16"),
+    "gt": ("sbuf", [128, 544], "bfloat16"),
+    "tt": ("sbuf", [128, 1056], "bfloat16"),
+    "pid": ("sbuf", [128, 2], "int32"),
+    "pat": ("sbuf", [128, 4], "int32"),
+    "k0": ("sbuf", [128, 8], "int32"),
+    "k1": ("sbuf", [128, 8], "float32"),
+    "pick": ("sbuf", [128, 32], "uint16"),
+    "dif": ("sbuf", [128, 128], "int32"),
+    "ident": ("sbuf", [128, 128], "bfloat16"),
+    "gs": ("sbuf", [128, 512 * 8], "bfloat16"),
+    "gl": ("sbuf", [128, 512 * 8], "bfloat16"),
+    "ys": ("sbuf", [128, 512], "float32"),
+    "ps": ("psum", [128, 512], "float32"),
+}
+SEMAPHORES = (["v", "a", "pe", "gi", "fac", "stg", "ray", "lay", "yd", "sent", "gf", "gd", "fa"]
+              + ["wl%d" % d for d in range(8)] + ["sa%d" % d for d in range(8)]
+              + ["st%d" % h for h in range(7)] + ["ix%d" % h for h in range(8)] + ["ga%d" % h for h in range(8)])
+
+
+def rank_program(g, core, T, topo):
+    rank = T.rank_of(core)
+    if rank is None:
+        return
+    S = T.sem
+    V, A, SY, PE = g.vector, g.scalar, g.sync, g.tensor
+    op = AluOpType
+    ACT = ActivationFunctionType
+    W = [T.w0, T.w1]
+
+    def peer(d):
+        return T.cores[(rank + d) % N]
+
+    def nbits(m):
+        return bin(m).count("1")
+
+    nv = [0, 0]
+
+    def vsync():
+        if nv[1] < nv[0]:
+            V.wait_ge(S.v, nv[0])
+            nv[1] = nv[0]
+
+    def vec(fn, dep=True):
+        if dep:
+            vsync()
+        fn().then_inc(S.v, 1)
+        nv[0] += 1
+        return nv[0]
+
+    na = [0, 0]
+
+    def act(fn, dep=True):
+        if dep and na[1] < na[0]:
+            A.wait_ge(S.a, na[0])
+            na[1] = na[0]
+        fn().then_inc(S.a, 1)
+        na[0] += 1
+        return na[0]
+
+    ts = V.tensor_scalar
+
+    SY.dma_start(T.fown[:], T.fac[:]).then_inc(S.fac, 16)
+    A.dma_start(T.stage[64:128, :], T.lay[15::16, :]).then_inc(S.stg, 16)
+    SY.dma_start(T.stage[0:64, :], T.lay[14::16, :]).then_inc(S.stg, 16)
+    A.dma_start(T.raw[:, 32:64], T.py[:]).then_inc(S.ray, 16)
+    SY.dma_start(T.raw[:, 0:32], T.px[:]).then_inc(S.ray, 16)
+    SY.dma_start(T.raw[:, 64:96], T.dx[:]).then_inc(S.ray, 16)
+    SY.dma_start(T.raw[:, 96:128], T.dy[:]).then_inc(S.ray, 16)
+    nlay = [0]
+
+    def load_lay(n):
+        for _ in range(n):
+            k = nlay[0]
+            SY.dma_start(T.ly[k::8, :], T.lay[k::8, :]).then_inc(S.lay, 16)
+            nlay[0] += 1
+
+    g.iota(T.pid[:, 0:1], [[1, 1]], 0, 17).then_inc(S.gi, 1)
+    g.iota(T.pid[:, 1:2], [[1, 1]], 0, 16).then_inc(S.gi, 1)
+    g.iota(T.pat[:], [[1, 2], [256, 2]], 0, 0).then_inc(S.gi, 1)
+    g.iota(T.w0[:, 7680:8192], [[0, 512]], 0, 0, allow_small_or_imprecise_dtypes=True).then_inc(S.gf, 1)
+    sent = [0]
+    g.wait_ge(S.fac, 16)
+    m0 = topo.mask(core, peer(-IMPORTS[0]))
+    ids = [topo.addr(peer(-d)) for d in IMPORTS]
+    g.remote_dma_fused([RemoteDMATransfer(dst_ids=[DstId(rid=i[0], pnc=i[1]) for i in ids], dma_engine_mask=m0,
+                                          remote_sem=S.fa, srcs=[T.fown[:]],
+                                          dsts=[T.fl[:, d:d + 1] for d in IMPORTS])], local_sem=S.sent)
+    sent[0] += nbits(m0)
+    nfa = sum(nbits(topo.mask(peer(d), peer(d - IMPORTS[0]))) for d in IMPORTS)
+
+    def put(out, in_, d, rsem):
+        rid, pid, _ = topo.addr(peer(d))
+        m = topo.mask(core, peer(d))
+        g.remote_dma(out, in_, rsem, S.sent, pid, rid, m)
+        sent[0] += nbits(m)
+
+    share = {n: len(c.split("+")) for c in G_ORDER for n in c.split("+")}
+
+    def cnt(d, name=None):
+        return nbits(topo.mask(peer(d), core)) // share.get(name, 1)
+
+    g.wait_ge(S.stg, 32)
+    put(T.land[0], T.stage[:], -IMPORTS[0], S["sa%d" % IMPORTS[0]])
+
+    f0 = vec(lambda: V.memset(T.w0[:, 0:1024], 0.0))
+    f1 = vec(lambda: V.memset(T.w0[:, 1024:5504], 0.0))
+    A.wait_ge(S.v, f0)
+    for a, b in ((5504, 6528), (6528, 7552), (7552, 7680)):
+        fa0 = act(lambda: A.activation(T.w0[:, a:b], T.w0[:, 0:b - a], ACT.Copy), dep=False)
+    SY.wait_ge(S.v, f1)
+    SY.wait_ge(S.a, fa0)
+    SY.wait_ge(S.gf, 1)
+    SY.dma_start(T.w0[0::16, :], T.lay[14::16, :]).then_inc(S.wl0, 16)
+    SY.dma_start(T.w0[1::16, :], T.lay[15::16, :]).then_inc(S.wl0, 16)
+    f2 = vec(lambda: V.memset(T.w1[:, 0:1024], 0.0))
+    A.wait_ge(S.v, f2)
+    for a in (1024, 2048):
+        fa1 = act(lambda: A.activation(T.w1[:, a:a + 1024], T.w1[:, 0:1024], ACT.Copy), dep=(a == 1024))
+
+    V.wait_ge(S.gi, 3)
+    vec(lambda: ts(T.k0[:, 0:1], T.pid[:, 0:1], 4, 1, op.arith_shift_right, op.bitwise_and))
+    vec(lambda: ts(T.k0[:, 1:2], T.pid[:, 1:2], 255, None, op.bitwise_and), dep=False)
+    vec(lambda: V.memset(T.gt[:, 0:16], 0.0), dep=False)
+    vec(lambda: V.memset(T.gt[:, 528:544], 0.0), dep=False)
+    vec(lambda: V.tensor_copy(T.k1[:, 0:1], T.k0[:, 1:2]))
+    vec(lambda: ts(T.k1[:, 1:2], T.k0[:, 0:1], 528.0, T.k1[:, 0:1], op.mult, op.add))
+    rows = sorted(set(w[1] for w in WIN.values()))
+    for i, rho in enumerate(rows):
+        vec(lambda: ts(T.pick[:, 4 * i:4 * i + 4], T.pat[:], T.k1[:, 1:2], float(rho), op.add, op.add), dep=(i == 0))
+    V.wait_ge(S.fac, 16)
+    vec(lambda: ts(T.fs0[:], T.fown[:], 1.0 / 16, None, op.mult), dep=False)
+    V.wait_ge(S.ray, 64)
+    vec(lambda: ts(T.hist[:, 0:64], T.raw[:, 0:64], 8.0, None, op.mult), dep=False)
+    vec(lambda: V.tensor_tensor(T.tw[:], T.raw[:, 0:64], T.raw[:, 64:128], op.add), dep=False)
+
+    def slot(k):
+        return T.hist[:, 64 * k:64 * k + 64]
+
+    def cells(k, h, stepping=True):
+        vec(lambda: ts(T.cx[:], T.hist[:, 64 * k:64 * k + 32], 7, 127, op.arith_shift_right, op.bitwise_and))
+        vec(lambda: ts(T.cy[:], T.hist[:, 64 * k + 32:64 * k + 64], 63 * 128, None, op.bitwise_and), dep=False)
+        vec(lambda: V.tensor_tensor(T.cell[:], T.cx[:], T.cy[:], op.add))
+        if h == 0:
+            vec(lambda: ts(T.pre[:], T.tw[:], 8.0, -BIAS, op.mult, op.add), dep=False)
+        elif stepping:
+            vec(lambda: ts(T.tw[:], slot(k), 2.0, -BIAS, op.mult, op.add), dep=False)
+        return vec(lambda: V.tensor_copy(T.ixl[:, 32 * h:32 * h + 32], T.cell[:]))
+
+    ready = {}
+    ixdone = {0: cells(0, 0)}
+
+    vseen, aseen = set(), set()
+
+    def gather_ready(Q, seen, h):
+        if "lay" not in seen:
+            Q.wait_ge(S.lay, 128)
+            seen.add("lay")
+        if (h < 7 and O[h] == h) or (h > 0 and O[h - 1] == h):
+            if Q is A:
+                A.wait_ge(S.v, ixdone[h])
+            return T.ixl
+        Q.wait_ge(S["ix%d" % h], cnt(O[h - 1] - h, "ix%d" % h))
+        return T.ixr
+
+    gdone = {}
+
+    def e_act(h, a=0, b=32):
+        buf = gather_ready(A, aseen, h)
+        return act(lambda: A.activation(T.gs[:, 512 * h + 16 * a:512 * h + 16 * b],
+                                        T.ly[:].indirect(buf[:, 32 * h + a:32 * h + b]), ACT.Copy))
+
+    def e_vec(h, a=0, b=32):
+        buf = gather_ready(V, vseen, h)
+        return vec(lambda: V.tensor_copy(T.gs[:, 512 * h + 16 * a:512 * h + 16 * b],
+                                         T.ly[:].indirect(buf[:, 32 * h + a:32 * h + b])))
+
+    cur = 0
+    hops = {}
+    gate = {}
+    stepdone = {}
+    for h in range(7):
+        d = (h - O[h]) % N
+        w, rho, _ = WIN[d]
+        if h > 0 and O[h] != O[h - 1]:
+            V.wait_ge(S["st%d" % (h - 1)], cnt(O[h - 1] - O[h]))
+            cur += 2
+            ixdone[h] = cells(cur, h)
+        for dd, (w2, _, gt) in WIN.items():
+            if w2 == w and (gt is None or gt < h):
+                for Q, seen in ((V, vseen), (A, aseen)):
+                    if ("w", dd) not in seen:
+                        Q.wait_ge(S["wl%d" % dd], 32)
+                        seen.add(("w", dd))
+        fsc = T.fs0[:] if d == 0 else T.fs[:, d:d + 1]
+        ix = T.ixl
+        sp = 16 if h == 0 else SPLIT
+        gv = vec(lambda: ts(T.gt[:, 16:16 + 16 * sp], W[w][:].indirect(ix[:, 32 * h:32 * h + sp]), fsc, RB,
+                            op.mult, op.add))
+        A.wait_ge(S.v, ixdone[h])
+        ga = act(lambda: A.activation(T.gt[:, 16 + 16 * sp:528], W[w][:].indirect(ix[:, 32 * h + sp:32 * h + 32]),
+                                      ACT.Identity, bias=RB, scale=fsc))
+        if h > 0:
+            gv = vec(lambda: V.tensor_tensor(T.pre[:], T.tw[:], slot(cur - 1), op.subtract), dep=False)
+        gate[h] = (gv, ga)
+        V.wait_ge(S.a, ga)
+        vec(lambda: V.transpose(T.tt[:, 0:512], T.gt[:, 16:528]))
+        vec(lambda: V.transpose(T.tt[:, 512:1056], T.gt[:, 0:544]), dep=False)
+        i = rows.index(rho)
+        pv = vec(lambda: V.tensor_tensor(slot(cur + 1), T.tt[:].indirect(T.pick[:, 4 * i:4 * i + 4]), T.pre[:], op.add))
+        cur += 1
+        stepdone[h] = pv
+        stay = h < 6 and O[h + 1] == O[h]
+        if h < 6 and not stay:
+            ready["st%d" % h] = [(S.v, pv)]
+            hops[h] = cur
+        if stay or h == 6 or O[h + 1] != h + 1:
+            n = cells(cur, h + 1, stay)
+            ixdone[h + 1] = n
+            ready["ix%d" % (h + 1)] = [(S.v, n)]
+        if h == 0:
+            f3 = vec(lambda: V.memset(T.w1[:, 5120:8192], 0.0))
+            for a in (3072, 4096):
+                fa1 = act(lambda: A.activation(T.w1[:, a:a + 1024], T.w1[:, 0:1024], ACT.Copy), dep=(a == 3072))
+            V.wait_ge(S.fa, nfa)
+            lo, hi = min(IMPORTS), max(IMPORTS) + 1
+            vec(lambda: ts(T.fs[:, lo:hi], T.fl[:, lo:hi], 1.0 / 16, None, op.mult))
+        if h == IDENT_AFTER:
+            V.wait_ge(S.gd, 1)
+            idn = vec(lambda: ts(T.ident[:], T.dif[:], 0.0, None, op.is_equal))
+            vsync()
+        for e in ACT_E.get(h, []):
+            gdone[e] = [(S.a, e_act(e))]
+        for e in DVE_E.get(h, []):
+            gdone[e] = [(S.v, e_vec(e))]
+    gdone[7] = [(S.a, e_act(7, 16, 32)), (S.v, e_vec(7, 0, 16))]
+    for h in range(1, 8):
+        ready["G%d" % h] = gdone[h]
+
+    def reload(d):
+        w, rho, gt = WIN[d]
+        i = IMPORTS.index(d)
+        SY.wait_ge(S["sa%d" % d], cnt(d))
+        if w == 1:
+            SY.wait_ge(S.v, f3)
+            SY.wait_ge(S.a, fa1)
+        if gt is not None:
+            SY.wait_ge(S.v, gate[gt][0])
+            SY.wait_ge(S.a, gate[gt][1])
+        SY.dma_start(W[w][rho::16, :], T.land[i, 0:64, :]).then_inc(S["wl%d" % d], 16)
+        SY.dma_start(W[w][rho + 1::16, :], T.land[i, 64:128, :]).then_inc(S["wl%d" % d], 16)
+
+    for what, x in SYNC_ORDER:
+        if what == "lay":
+            load_lay(x)
+        elif what == "win":
+            reload(x)
+        elif what == "gather":
+            SY.wait_ge(S.v, gate[x][0])
+        else:
+            SY.wait_ge(S.v, stepdone[x])
+
+    for name in G_ORDER:
+        if name == "id":
+            g.iota(T.dif[:], [[1, 128]], 0, -1).then_inc(S.gd, 1)
+            continue
+        h = int(name[-1])
+        if name[:2] == "sl":
+            put(T.land[IMPORTS.index(h)], T.stage[:], -h, S["sa%d" % h])
+            continue
+        parts = []
+        for nm in name.split("+"):
+            for s, n in ready[nm]:
+                g.wait_ge(s, n)
+            h = int(nm[-1])
+            if nm[0] == "s":
+                k = hops[h]
+                parts.append((T.hist[:, 64 * (k + 1):64 * (k + 3)], T.hist[:, 64 * (k - 1):64 * (k + 1)],
+                              O[h + 1] - O[h], S[nm]))
+            elif nm[0] == "i":
+                parts.append((T.ixr[:, 32 * h:32 * h + 32], T.ixl[:, 32 * h:32 * h + 32], h - O[h - 1], S[nm]))
+            else:
+                parts.append((T.gl[:, 512 * h:512 * h + 512], T.gs[:, 512 * h:512 * h + 512], -h, S["ga%d" % h]))
+        if len(parts) == 1:
+            put(*parts[0])
+            continue
+        trs = []
+        for j, (out, in_, d, rsem) in enumerate(parts):
+            en = topo.engines(core, peer(d))
+            en = en[j * len(en) // len(parts):(j + 1) * len(en) // len(parts)]
+            rid, pid, _ = topo.addr(peer(d))
+            trs.append(RemoteDMATransfer(dst_ids=[DstId(rid=rid, pnc=pid)], dma_engine_mask=sum(1 << e for e in en),
+                                         remote_sem=rsem, srcs=[in_], dsts=[out]))
+            sent[0] += len(en)
+        g.remote_dma_fused(trs, local_sem=S.sent)
+    g.wait_ge(S.sent, sent[0])
+
+    PE.wait_ge(S.v, idn)
+    for j, h in enumerate(PE_ORDER):
+        if h == 0:
+            for s, n in gdone[0]:
+                PE.wait_ge(s, n)
+            src = T.gs[:, 0:512]
+        else:
+            PE.wait_ge(S["ga%d" % h], cnt(h, "G%d" % h))
+            src = T.gl[:, 512 * h:512 * h + 512]
+        mm = PE.matmul(T.ps[:], T.ident[:], src, j == 0, j == 6)
+    mm.then_inc(S.pe, 1)
+    V.wait_ge(S.pe, 1)
+    V.wait_ge(S.ga7, cnt(7, "G7"))
+    n = vec(lambda: V.tensor_tensor(T.ys[:], T.ps[:], T.gl[:, 3584:4096], op.add))
+    SY.wait_ge(S.v, n)
+    SY.dma_start(T.y[:], T.ys[:]).then_inc(S.yd, 16)
+    SY.wait_ge(S.yd, 16)

@@ -3,16 +3,19 @@ from concourse.mybir import AluOpType, ActivationFunctionType
 
 N = 8
 C = 8192
-O = [0, 1, 1, 1, 4, 4, 4]
-WIN = {0: (0, 0, None), 1: (1, 0, None), 2: (0, 2, 1)}
-IMPORTS = [1, 2]
-ACT_E = {4: [1], 5: [2], 6: [3, 4, 5]}
-DVE_E = {6: [0, 6]}
-G_ORDER = "st0 sl2 id st3 ix2+ix3 ix5 G1 ix6 G2 ix7 G3 G4 G5 G6 G7".split()
-SYNC_ORDER = [("lay", 1), ("done", 0), ("lay", 1), ("win", 1), ("lay", 1), ("win", 2), ("lay", 3), ("done", 3), ("lay", 2)]
-PE_ORDER = [1, 2, 0, 3, 4, 5, 6]
-IDENT_AFTER = 3
-SPLIT = 14
+O = [0, 4, 4, 4, 4, 7, 7, 7]
+OWN = 14
+WIN = {0: (0, OWN, None), 5: (0, 0, 0), 6: (1, 0, None), 7: (0, 2, 1)}
+IMPORTS = [5, 6, 7]
+PRE = 2048
+ACT_E = {4: [1, 2, 3], 5: [0], 6: [5, 6]}
+DVE_E = {4: [4], 6: [7]}
+G_ORDER = "sl5 sl6 st0 sl7 id ix1+ix2+ix3 st4 G1+G4 G2+G3 ix5 ix6 G5 G6+G7".split()
+SYNC_ORDER = [("lay", 1), ("sem", "wl0"), ("lay", 1), ("win", 5), ("sem", "st0"), ("lay", 1), ("win", 6), ("lay", 1),
+              ("win", 7), ("lay", 4)]
+PE_ORDER = [1, 4, 2, 3, 0, 5, 6]
+IDENT_AFTER = 4
+SPLIT = 16
 BIAS = 1536.0
 RB = BIAS - 127.0 / 32.0
 
@@ -21,13 +24,13 @@ SCRATCH = {
     "w0": ("sbuf", [128, C], "bfloat16"),
     "w1": ("sbuf", [128, C], "bfloat16"),
     "stage": ("dram", [128, 1024], "bfloat16"),
-    "land": ("dram", [7, 128, 1024], "bfloat16"),
+    "land": ("dram", [3, 128, 1024], "bfloat16"),
     "fown": ("sbuf", [128, 1], "int32"),
     "fl": ("sbuf", [128, 8], "int32"),
     "fs0": ("sbuf", [128, 1], "float32"),
     "fs": ("sbuf", [128, 8], "float32"),
     "raw": ("sbuf", [128, 128], "int32"),
-    "hist": ("sbuf", [128, 64 * 24], "int32"),
+    "hist": ("sbuf", [128, 64 * 16], "int32"),
     "pre": ("sbuf", [128, 64], "float32"),
     "tw": ("sbuf", [128, 64], "float32"),
     "cx": ("sbuf", [128, 32], "int32"),
@@ -67,32 +70,21 @@ def rank_program(g, core, T, topo):
     def peer(d):
         return T.cores[(rank + d) % N]
 
-    def nbits(m):
-        return bin(m).count("1")
+    nv, na = [0, 0], [0, 0]
 
-    nv = [0, 0]
+    def issue(Q, sem, n, fn, after):
+        if after > n[1]:
+            Q.wait_ge(sem, after)
+            n[1] = after
+        fn().then_inc(sem, 1)
+        n[0] += 1
+        return n[0]
 
-    def vsync():
-        if nv[1] < nv[0]:
-            V.wait_ge(S.v, nv[0])
-            nv[1] = nv[0]
+    def vec(fn, after=0):
+        return issue(V, S.v, nv, fn, after)
 
-    def vec(fn, dep=True):
-        if dep:
-            vsync()
-        fn().then_inc(S.v, 1)
-        nv[0] += 1
-        return nv[0]
-
-    na = [0, 0]
-
-    def act(fn, dep=True):
-        if dep and na[1] < na[0]:
-            A.wait_ge(S.a, na[0])
-            na[1] = na[0]
-        fn().then_inc(S.a, 1)
-        na[0] += 1
-        return na[0]
+    def act(fn, after=0):
+        return issue(A, S.a, na, fn, after)
 
     ts = V.tensor_scalar
 
@@ -103,6 +95,7 @@ def rank_program(g, core, T, topo):
     SY.dma_start(T.raw[:, 0:32], T.px[:]).then_inc(S.ray, 16)
     SY.dma_start(T.raw[:, 64:96], T.dx[:]).then_inc(S.ray, 16)
     SY.dma_start(T.raw[:, 96:128], T.dy[:]).then_inc(S.ray, 16)
+    SY.dma_start(T.w0[:, 0:PRE], T.lay[:, 0:PRE]).then_inc(S.wl0, 16)
     nlay = [0]
 
     def load_lay(n):
@@ -111,80 +104,94 @@ def rank_program(g, core, T, topo):
             SY.dma_start(T.ly[k::8, :], T.lay[k::8, :]).then_inc(S.lay, 16)
             nlay[0] += 1
 
+    def deal(src, dst, j, n):
+        en = topo.engines(src, dst)
+        cuts = {1: [0, 4], 2: [0, 2, 4], 3: [0, 1, 2, 4]}[n]
+        return en[cuts[j] * len(en) // 4:cuts[j + 1] * len(en) // 4]
+
+    place = {nm: (j, len(c.split("+"))) for c in G_ORDER for j, nm in enumerate(c.split("+"))}
+
+    def cnt(d, name=None):
+        return len(deal(peer(d), core, *place.get(name, (0, 1))))
+
+    sent = [0]
+
+    def put(parts):
+        trs = []
+        for j, (out, in_, d, rsem) in enumerate(parts):
+            en = deal(core, peer(d), j, len(parts))
+            rid, pid, _ = topo.addr(peer(d))
+            sent[0] += len(en)
+            if len(parts) == 1:
+                g.remote_dma(out, in_, rsem, S.sent, pid, rid, topo.mask(core, peer(d)))
+                return
+            trs.append(RemoteDMATransfer(dst_ids=[DstId(rid=rid, pnc=pid)], dma_engine_mask=sum(1 << e for e in en),
+                                         remote_sem=rsem, srcs=[in_], dsts=[out]))
+        g.remote_dma_fused(trs, local_sem=S.sent)
+
     g.iota(T.pid[:, 0:1], [[1, 1]], 0, 17).then_inc(S.gi, 1)
     g.iota(T.pid[:, 1:2], [[1, 1]], 0, 16).then_inc(S.gi, 1)
     g.iota(T.pat[:], [[1, 2], [256, 2]], 0, 0).then_inc(S.gi, 1)
     g.iota(T.w0[:, 7680:8192], [[0, 512]], 0, 0, allow_small_or_imprecise_dtypes=True).then_inc(S.gf, 1)
-    sent = [0]
     g.wait_ge(S.fac, 16)
     m0 = topo.mask(core, peer(-IMPORTS[0]))
     ids = [topo.addr(peer(-d)) for d in IMPORTS]
     g.remote_dma_fused([RemoteDMATransfer(dst_ids=[DstId(rid=i[0], pnc=i[1]) for i in ids], dma_engine_mask=m0,
                                           remote_sem=S.fa, srcs=[T.fown[:]],
                                           dsts=[T.fl[:, d:d + 1] for d in IMPORTS])], local_sem=S.sent)
-    sent[0] += nbits(m0)
-    nfa = sum(nbits(topo.mask(peer(d), peer(d - IMPORTS[0]))) for d in IMPORTS)
-
-    def put(out, in_, d, rsem):
-        rid, pid, _ = topo.addr(peer(d))
-        m = topo.mask(core, peer(d))
-        g.remote_dma(out, in_, rsem, S.sent, pid, rid, m)
-        sent[0] += nbits(m)
-
-    share = {n: len(c.split("+")) for c in G_ORDER for n in c.split("+")}
-
-    def cnt(d, name=None):
-        return nbits(topo.mask(peer(d), core)) // share.get(name, 1)
-
+    sent[0] += len(topo.engines(core, peer(-IMPORTS[0])))
+    nfa = sum(len(topo.engines(peer(d), peer(d - IMPORTS[0]))) for d in IMPORTS)
     g.wait_ge(S.stg, 32)
-    put(T.land[0], T.stage[:], -IMPORTS[0], S["sa%d" % IMPORTS[0]])
 
-    f0 = vec(lambda: V.memset(T.w0[:, 0:1024], 0.0))
-    f1 = vec(lambda: V.memset(T.w0[:, 1024:5504], 0.0))
+    f0 = vec(lambda: V.memset(T.w0[:, PRE:PRE + 512], 0.0))
+    f1 = vec(lambda: V.memset(T.w0[:, PRE + 512:6144], 0.0))
     A.wait_ge(S.v, f0)
-    for a, b in ((5504, 6528), (6528, 7552), (7552, 7680)):
-        fa0 = act(lambda: A.activation(T.w0[:, a:b], T.w0[:, 0:b - a], ACT.Copy), dep=False)
-    SY.wait_ge(S.v, f1)
-    SY.wait_ge(S.a, fa0)
-    SY.wait_ge(S.gf, 1)
-    SY.dma_start(T.w0[0::16, :], T.lay[14::16, :]).then_inc(S.wl0, 16)
-    SY.dma_start(T.w0[1::16, :], T.lay[15::16, :]).then_inc(S.wl0, 16)
+    for a in (6144, 6656, 7168):
+        fa0 = act(lambda: A.activation(T.w0[:, a:a + 512], T.w0[:, PRE:PRE + 512], ACT.Copy))
+    for Q, row in ((SY, OWN), (A, OWN + 1)):
+        Q.wait_ge(S.v, f1)
+        Q.wait_ge(S.a, fa0)
+        Q.wait_ge(S.gf, 1)
+        Q.dma_start(T.w0[row::16, PRE:], T.lay[row::16, PRE:]).then_inc(S.wl0, 16)
+    na[1] = fa0
+    loads = {d: 32 for d in IMPORTS}
+    loads[0] = 48
     f2 = vec(lambda: V.memset(T.w1[:, 0:1024], 0.0))
     A.wait_ge(S.v, f2)
     for a in (1024, 2048):
-        fa1 = act(lambda: A.activation(T.w1[:, a:a + 1024], T.w1[:, 0:1024], ACT.Copy), dep=(a == 1024))
+        fa1 = act(lambda: A.activation(T.w1[:, a:a + 1024], T.w1[:, 0:1024], ACT.Copy))
 
     V.wait_ge(S.gi, 3)
     vec(lambda: ts(T.k0[:, 0:1], T.pid[:, 0:1], 4, 1, op.arith_shift_right, op.bitwise_and))
-    vec(lambda: ts(T.k0[:, 1:2], T.pid[:, 1:2], 255, None, op.bitwise_and), dep=False)
-    vec(lambda: V.memset(T.gt[:, 0:16], 0.0), dep=False)
-    vec(lambda: V.memset(T.gt[:, 528:544], 0.0), dep=False)
-    vec(lambda: V.tensor_copy(T.k1[:, 0:1], T.k0[:, 1:2]))
-    vec(lambda: ts(T.k1[:, 1:2], T.k0[:, 0:1], 528.0, T.k1[:, 0:1], op.mult, op.add))
+    n = vec(lambda: ts(T.k0[:, 1:2], T.pid[:, 1:2], 255, None, op.bitwise_and))
+    vec(lambda: V.memset(T.gt[:, 0:16], 0.0))
+    vec(lambda: V.memset(T.gt[:, 528:544], 0.0))
+    n = vec(lambda: V.tensor_copy(T.k1[:, 0:1], T.k0[:, 1:2]), n)
+    n = vec(lambda: ts(T.k1[:, 1:2], T.k0[:, 0:1], 528.0, T.k1[:, 0:1], op.mult, op.add), n)
     rows = sorted(set(w[1] for w in WIN.values()))
     for i, rho in enumerate(rows):
-        vec(lambda: ts(T.pick[:, 4 * i:4 * i + 4], T.pat[:], T.k1[:, 1:2], float(rho), op.add, op.add), dep=(i == 0))
+        vec(lambda: ts(T.pick[:, 4 * i:4 * i + 4], T.pat[:], T.k1[:, 1:2], float(rho), op.add, op.add), n)
     V.wait_ge(S.fac, 16)
-    vec(lambda: ts(T.fs0[:], T.fown[:], 1.0 / 16, None, op.mult), dep=False)
+    vec(lambda: ts(T.fs0[:], T.fown[:], 1.0 / 16, None, op.mult))
     V.wait_ge(S.ray, 64)
-    vec(lambda: ts(T.hist[:, 0:64], T.raw[:, 0:64], 8.0, None, op.mult), dep=False)
-    vec(lambda: V.tensor_tensor(T.tw[:], T.raw[:, 0:64], T.raw[:, 64:128], op.add), dep=False)
+    n = vec(lambda: ts(T.hist[:, 0:64], T.raw[:, 0:64], 8.0, None, op.mult))
+    vec(lambda: V.tensor_tensor(T.tw[:], T.raw[:, 0:64], T.raw[:, 64:128], op.add))
 
-    def slot(k):
-        return T.hist[:, 64 * k:64 * k + 64]
+    def slot(k, a=0, b=64):
+        return T.hist[:, 64 * k + a:64 * k + b]
 
-    def cells(k, h, stepping=True):
-        vec(lambda: ts(T.cx[:], T.hist[:, 64 * k:64 * k + 32], 7, 127, op.arith_shift_right, op.bitwise_and))
-        vec(lambda: ts(T.cy[:], T.hist[:, 64 * k + 32:64 * k + 64], 63 * 128, None, op.bitwise_and), dep=False)
-        vec(lambda: V.tensor_tensor(T.cell[:], T.cx[:], T.cy[:], op.add))
+    def cells(k, h, after):
+        vec(lambda: ts(T.cx[:], slot(k, 0, 32), 7, 127, op.arith_shift_right, op.bitwise_and), after)
+        n = vec(lambda: ts(T.cy[:], slot(k, 32, 64), 63 * 128, None, op.bitwise_and))
+        if 0 < h < 7:
+            vec(lambda: ts(T.tw[:], slot(k), 2.0, -BIAS, op.mult, op.add))
+        n = vec(lambda: V.tensor_tensor(T.cell[:], T.cx[:], T.cy[:], op.add), n)
         if h == 0:
-            vec(lambda: ts(T.pre[:], T.tw[:], 8.0, -BIAS, op.mult, op.add), dep=False)
-        elif stepping:
-            vec(lambda: ts(T.tw[:], slot(k), 2.0, -BIAS, op.mult, op.add), dep=False)
-        return vec(lambda: V.tensor_copy(T.ixl[:, 32 * h:32 * h + 32], T.cell[:]))
+            vec(lambda: ts(T.pre[:], T.tw[:], 8.0, -BIAS, op.mult, op.add))
+        return vec(lambda: V.tensor_copy(T.ixl[:, 32 * h:32 * h + 32], T.cell[:]), n)
 
     ready = {}
-    ixdone = {0: cells(0, 0)}
+    ixdone = {0: cells(0, 0, n)}
 
     vseen, aseen = set(), set()
 
@@ -192,84 +199,85 @@ def rank_program(g, core, T, topo):
         if "lay" not in seen:
             Q.wait_ge(S.lay, 128)
             seen.add("lay")
-        if (h < 7 and O[h] == h) or (h > 0 and O[h - 1] == h):
+        if O[h] == h:
             if Q is A:
                 A.wait_ge(S.v, ixdone[h])
             return T.ixl
-        Q.wait_ge(S["ix%d" % h], cnt(O[h - 1] - h, "ix%d" % h))
+        Q.wait_ge(S["ix%d" % h], cnt(O[h] - h, "ix%d" % h))
         return T.ixr
 
     gdone = {}
 
-    def e_act(h, a=0, b=32):
+    def e_act(h):
         buf = gather_ready(A, aseen, h)
-        return act(lambda: A.activation(T.gs[:, 512 * h + 16 * a:512 * h + 16 * b],
-                                        T.ly[:].indirect(buf[:, 32 * h + a:32 * h + b]), ACT.Copy))
+        return act(lambda: A.activation(T.gs[:, 512 * h:512 * h + 512],
+                                        T.ly[:].indirect(buf[:, 32 * h:32 * h + 32]), ACT.Copy))
 
-    def e_vec(h, a=0, b=32):
+    def e_vec(h):
         buf = gather_ready(V, vseen, h)
-        return vec(lambda: V.tensor_copy(T.gs[:, 512 * h + 16 * a:512 * h + 16 * b],
-                                         T.ly[:].indirect(buf[:, 32 * h + a:32 * h + b])))
+        return vec(lambda: V.tensor_copy(T.gs[:, 512 * h:512 * h + 512],
+                                         T.ly[:].indirect(buf[:, 32 * h:32 * h + 32])), ixdone.get(h, 0))
 
     cur = 0
     hops = {}
     gate = {}
-    stepdone = {}
     for h in range(7):
         d = (h - O[h]) % N
         w, rho, _ = WIN[d]
         if h > 0 and O[h] != O[h - 1]:
             V.wait_ge(S["st%d" % (h - 1)], cnt(O[h - 1] - O[h]))
             cur += 2
-            ixdone[h] = cells(cur, h)
+            ixdone[h] = cells(cur, h, pv)
+            ready["ix%d" % h] = [(S.v, ixdone[h])]
         for dd, (w2, _, gt) in WIN.items():
             if w2 == w and (gt is None or gt < h):
                 for Q, seen in ((V, vseen), (A, aseen)):
                     if ("w", dd) not in seen:
-                        Q.wait_ge(S["wl%d" % dd], 32)
+                        Q.wait_ge(S["wl%d" % dd], loads[dd])
                         seen.add(("w", dd))
         fsc = T.fs0[:] if d == 0 else T.fs[:, d:d + 1]
         ix = T.ixl
-        sp = 16 if h == 0 else SPLIT
-        gv = vec(lambda: ts(T.gt[:, 16:16 + 16 * sp], W[w][:].indirect(ix[:, 32 * h:32 * h + sp]), fsc, RB,
-                            op.mult, op.add))
+
+        def pre(a, b):
+            if h > 0:
+                vec(lambda: V.tensor_tensor(T.pre[:, a:b], T.tw[:, a:b], slot(cur - 1, a, b), op.subtract))
+
+        pre(0, 32)
+        gv = vec(lambda: ts(T.gt[:, 16:16 + 16 * SPLIT], W[w][:].indirect(ix[:, 32 * h:32 * h + SPLIT]), fsc, RB,
+                            op.mult, op.add), ixdone[h])
         A.wait_ge(S.v, ixdone[h])
-        ga = act(lambda: A.activation(T.gt[:, 16 + 16 * sp:528], W[w][:].indirect(ix[:, 32 * h + sp:32 * h + 32]),
+        ga = act(lambda: A.activation(T.gt[:, 16 + 16 * SPLIT:528],
+                                      W[w][:].indirect(ix[:, 32 * h + SPLIT:32 * h + 32]),
                                       ACT.Identity, bias=RB, scale=fsc))
-        if h > 0:
-            gv = vec(lambda: V.tensor_tensor(T.pre[:], T.tw[:], slot(cur - 1), op.subtract), dep=False)
+        pre(32, 64)
         gate[h] = (gv, ga)
         V.wait_ge(S.a, ga)
-        vec(lambda: V.transpose(T.tt[:, 0:512], T.gt[:, 16:528]))
-        vec(lambda: V.transpose(T.tt[:, 512:1056], T.gt[:, 0:544]), dep=False)
+        vec(lambda: V.transpose(T.tt[:, 0:512], T.gt[:, 16:528]), gv)
+        n = vec(lambda: V.transpose(T.tt[:, 512:1056], T.gt[:, 0:544]))
         i = rows.index(rho)
-        pv = vec(lambda: V.tensor_tensor(slot(cur + 1), T.tt[:].indirect(T.pick[:, 4 * i:4 * i + 4]), T.pre[:], op.add))
+        pv = vec(lambda: V.tensor_tensor(slot(cur + 1), T.tt[:].indirect(T.pick[:, 4 * i:4 * i + 4]), T.pre[:],
+                                         op.add), n)
         cur += 1
-        stepdone[h] = pv
-        stay = h < 6 and O[h + 1] == O[h]
-        if h < 6 and not stay:
+        if O[h + 1] == O[h]:
+            ixdone[h + 1] = cells(cur, h + 1, pv)
+            ready["ix%d" % (h + 1)] = [(S.v, ixdone[h + 1])]
+        else:
             ready["st%d" % h] = [(S.v, pv)]
             hops[h] = cur
-        if stay or h == 6 or O[h + 1] != h + 1:
-            n = cells(cur, h + 1, stay)
-            ixdone[h + 1] = n
-            ready["ix%d" % (h + 1)] = [(S.v, n)]
         if h == 0:
             f3 = vec(lambda: V.memset(T.w1[:, 5120:8192], 0.0))
             for a in (3072, 4096):
-                fa1 = act(lambda: A.activation(T.w1[:, a:a + 1024], T.w1[:, 0:1024], ACT.Copy), dep=(a == 3072))
+                fa1 = act(lambda: A.activation(T.w1[:, a:a + 1024], T.w1[:, 0:1024], ACT.Copy))
             V.wait_ge(S.fa, nfa)
             lo, hi = min(IMPORTS), max(IMPORTS) + 1
-            vec(lambda: ts(T.fs[:, lo:hi], T.fl[:, lo:hi], 1.0 / 16, None, op.mult))
+            pv = vec(lambda: ts(T.fs[:, lo:hi], T.fl[:, lo:hi], 1.0 / 16, None, op.mult))
         if h == IDENT_AFTER:
             V.wait_ge(S.gd, 1)
             idn = vec(lambda: ts(T.ident[:], T.dif[:], 0.0, None, op.is_equal))
-            vsync()
         for e in ACT_E.get(h, []):
             gdone[e] = [(S.a, e_act(e))]
         for e in DVE_E.get(h, []):
             gdone[e] = [(S.v, e_vec(e))]
-    gdone[7] = [(S.a, e_act(7, 16, 32)), (S.v, e_vec(7, 0, 16))]
     for h in range(1, 8):
         ready["G%d" % h] = gdone[h]
 
@@ -291,44 +299,32 @@ def rank_program(g, core, T, topo):
             load_lay(x)
         elif what == "win":
             reload(x)
-        elif what == "gather":
-            SY.wait_ge(S.v, gate[x][0])
+        elif x == "wl0":
+            SY.wait_ge(S.wl0, loads[0])
         else:
-            SY.wait_ge(S.v, stepdone[x])
+            h = int(x[-1])
+            SY.wait_ge(S[x], cnt(O[h] - O[h + 1]))
 
     for name in G_ORDER:
         if name == "id":
             g.iota(T.dif[:], [[1, 128]], 0, -1).then_inc(S.gd, 1)
             continue
-        h = int(name[-1])
-        if name[:2] == "sl":
-            put(T.land[IMPORTS.index(h)], T.stage[:], -h, S["sa%d" % h])
-            continue
         parts = []
         for nm in name.split("+"):
-            for s, n in ready[nm]:
+            for s, n in ready.get(nm, []):
                 g.wait_ge(s, n)
             h = int(nm[-1])
-            if nm[0] == "s":
+            if nm[:2] == "sl":
+                parts.append((T.land[IMPORTS.index(h)], T.stage[:], -h, S["sa%d" % h]))
+            elif nm[:2] == "st":
                 k = hops[h]
                 parts.append((T.hist[:, 64 * (k + 1):64 * (k + 3)], T.hist[:, 64 * (k - 1):64 * (k + 1)],
                               O[h + 1] - O[h], S[nm]))
-            elif nm[0] == "i":
-                parts.append((T.ixr[:, 32 * h:32 * h + 32], T.ixl[:, 32 * h:32 * h + 32], h - O[h - 1], S[nm]))
+            elif nm[:2] == "ix":
+                parts.append((T.ixr[:, 32 * h:32 * h + 32], T.ixl[:, 32 * h:32 * h + 32], h - O[h], S[nm]))
             else:
                 parts.append((T.gl[:, 512 * h:512 * h + 512], T.gs[:, 512 * h:512 * h + 512], -h, S["ga%d" % h]))
-        if len(parts) == 1:
-            put(*parts[0])
-            continue
-        trs = []
-        for j, (out, in_, d, rsem) in enumerate(parts):
-            en = topo.engines(core, peer(d))
-            en = en[j * len(en) // len(parts):(j + 1) * len(en) // len(parts)]
-            rid, pid, _ = topo.addr(peer(d))
-            trs.append(RemoteDMATransfer(dst_ids=[DstId(rid=rid, pnc=pid)], dma_engine_mask=sum(1 << e for e in en),
-                                         remote_sem=rsem, srcs=[in_], dsts=[out]))
-            sent[0] += len(en)
-        g.remote_dma_fused(trs, local_sem=S.sent)
+        put(parts)
     g.wait_ge(S.sent, sent[0])
 
     PE.wait_ge(S.v, idn)
@@ -344,7 +340,8 @@ def rank_program(g, core, T, topo):
     mm.then_inc(S.pe, 1)
     V.wait_ge(S.pe, 1)
     V.wait_ge(S.ga7, cnt(7, "G7"))
-    n = vec(lambda: V.tensor_tensor(T.ys[:], T.ps[:], T.gl[:, 3584:4096], op.add))
-    SY.wait_ge(S.v, n)
-    SY.dma_start(T.y[:], T.ys[:]).then_inc(S.yd, 16)
-    SY.wait_ge(S.yd, 16)
+    for Q, a in ((SY, 0), (A, 256)):
+        n = vec(lambda: V.tensor_tensor(T.ys[:, a:a + 256], T.ps[:, a:a + 256], T.gl[:, 3584 + a:3840 + a], op.add))
+        Q.wait_ge(S.v, n)
+        Q.dma_start(T.y[:, a:a + 256], T.ys[:, a:a + 256]).then_inc(S.yd, 16)
+    SY.wait_ge(S.yd, 32)

@@ -4,18 +4,25 @@ from concourse.mybir import AluOpType, ActivationFunctionType
 N = 8
 C = 8192
 O = [0, 4, 4, 4, 4, 7, 7, 7]
+EARLY = [5]
 OWN = 14
 WIN = {0: (0, OWN, None), 5: (0, 0, 0), 6: (1, 0, None), 7: (0, 2, 1)}
 IMPORTS = [5, 6, 7]
-PRE = 2048
-ACT_E = {4: [1, 2, 3], 5: [0], 6: [5, 6]}
-DVE_E = {4: [4], 6: [7]}
-G_ORDER = "sl5 sl6 st0 sl7 id ix1+ix2+ix3 st4 G1+G4 G2+G3 ix5 ix6 G5 G6+G7".split()
-SYNC_ORDER = [("lay", 1), ("sem", "wl0"), ("lay", 1), ("win", 5), ("sem", "st0"), ("lay", 1), ("win", 6), ("lay", 1),
-              ("win", 7), ("lay", 4)]
-PE_ORDER = [1, 4, 2, 3, 0, 5, 6]
+PRE = 1536
+FILL0 = (576, 3, 512)
+FILL1 = (2560, 4608)
+SY_HEAD = "fac stx px dx dy pre".split()
+ACT_HEAD = "sty py".split()
+ACT_E = {4: [1, 2], 5: [3], 6: [5]}
+DVE_E = {4: [4]}
+LAST = [7, 6, 0]
+FINAL = 6
+G_ORDER = "sl5 sl6 st0 sl7 id ix1+ix2 ix3 st4 ix5 G1+G4 G2 ix6 G3 G5 G7 G6".split()
+SYNC_ORDER = [("sem", "wl0"), ("lay", 1), ("win", 5), ("win", 6), ("lay", 2), ("win", 7), ("lay", 2), ("gate", 2),
+              ("lay", 3)]
+PE_ORDER = [1, 4, 2, 3, 0, 5, 7]
 IDENT_AFTER = 4
-SPLIT = 16
+SPLIT = 12
 BIAS = 1536.0
 RB = BIAS - 127.0 / 32.0
 
@@ -35,8 +42,7 @@ SCRATCH = {
     "tw": ("sbuf", [128, 64], "float32"),
     "cx": ("sbuf", [128, 32], "int32"),
     "cy": ("sbuf", [128, 32], "int32"),
-    "cell": ("sbuf", [128, 32], "int32"),
-    "ixl": ("sbuf", [128, 32 * 8], "uint16"),
+    "ixl": ("sbuf", [128, 32 * 9], "uint16"),
     "ixr": ("sbuf", [128, 32 * 8], "uint16"),
     "gt": ("sbuf", [128, 544], "bfloat16"),
     "tt": ("sbuf", [128, 1056], "bfloat16"),
@@ -70,6 +76,9 @@ def rank_program(g, core, T, topo):
     def peer(d):
         return T.cores[(rank + d) % N]
 
+    def made(h):
+        return O[h - 1] if h in EARLY else O[h]
+
     nv, na = [0, 0], [0, 0]
 
     def issue(Q, sem, n, fn, after):
@@ -88,14 +97,14 @@ def rank_program(g, core, T, topo):
 
     ts = V.tensor_scalar
 
-    SY.dma_start(T.fown[:], T.fac[:]).then_inc(S.fac, 16)
-    A.dma_start(T.stage[64:128, :], T.lay[15::16, :]).then_inc(S.stg, 16)
-    SY.dma_start(T.stage[0:64, :], T.lay[14::16, :]).then_inc(S.stg, 16)
-    A.dma_start(T.raw[:, 32:64], T.py[:]).then_inc(S.ray, 16)
-    SY.dma_start(T.raw[:, 0:32], T.px[:]).then_inc(S.ray, 16)
-    SY.dma_start(T.raw[:, 64:96], T.dx[:]).then_inc(S.ray, 16)
-    SY.dma_start(T.raw[:, 96:128], T.dy[:]).then_inc(S.ray, 16)
-    SY.dma_start(T.w0[:, 0:PRE], T.lay[:, 0:PRE]).then_inc(S.wl0, 16)
+    first = {"fac": (T.fown[:], T.fac[:], S.fac),
+             "stx": (T.stage[0:64, :], T.lay[14::16, :], S.stg), "sty": (T.stage[64:128, :], T.lay[15::16, :], S.stg),
+             "px": (T.raw[:, 0:32], T.px[:], S.ray), "py": (T.raw[:, 32:64], T.py[:], S.ray),
+             "dx": (T.raw[:, 64:96], T.dx[:], S.ray), "dy": (T.raw[:, 96:128], T.dy[:], S.ray),
+             "pre": (T.w0[:, 0:PRE], T.lay[:, 0:PRE], S.wl0)}
+    for Q, names in ((SY, SY_HEAD), (A, ACT_HEAD)):
+        for nm in names:
+            Q.dma_start(first[nm][0], first[nm][1]).then_inc(first[nm][2], 16)
     nlay = [0]
 
     def load_lay(n):
@@ -129,10 +138,11 @@ def rank_program(g, core, T, topo):
                                          remote_sem=rsem, srcs=[in_], dsts=[out]))
         g.remote_dma_fused(trs, local_sem=S.sent)
 
+    wa, nA, wg = FILL0
+    g.iota(T.w0[:, C - wg:C], [[0, wg]], 0, 0, allow_small_or_imprecise_dtypes=True).then_inc(S.gf, 1)
     g.iota(T.pid[:, 0:1], [[1, 1]], 0, 17).then_inc(S.gi, 1)
     g.iota(T.pid[:, 1:2], [[1, 1]], 0, 16).then_inc(S.gi, 1)
     g.iota(T.pat[:], [[1, 2], [256, 2]], 0, 0).then_inc(S.gi, 1)
-    g.iota(T.w0[:, 7680:8192], [[0, 512]], 0, 0, allow_small_or_imprecise_dtypes=True).then_inc(S.gf, 1)
     g.wait_ge(S.fac, 16)
     m0 = topo.mask(core, peer(-IMPORTS[0]))
     ids = [topo.addr(peer(-d)) for d in IMPORTS]
@@ -143,11 +153,12 @@ def rank_program(g, core, T, topo):
     nfa = sum(len(topo.engines(peer(d), peer(d - IMPORTS[0]))) for d in IMPORTS)
     g.wait_ge(S.stg, 32)
 
-    f0 = vec(lambda: V.memset(T.w0[:, PRE:PRE + 512], 0.0))
-    f1 = vec(lambda: V.memset(T.w0[:, PRE + 512:6144], 0.0))
+    va = C - wg - nA * wa
+    f0 = vec(lambda: V.memset(T.w0[:, PRE:PRE + wa], 0.0))
+    f1 = vec(lambda: V.memset(T.w0[:, PRE + wa:va], 0.0))
     A.wait_ge(S.v, f0)
-    for a in (6144, 6656, 7168):
-        fa0 = act(lambda: A.activation(T.w0[:, a:a + 512], T.w0[:, PRE:PRE + 512], ACT.Copy))
+    for a in range(va, C - wg, wa):
+        fa0 = act(lambda: A.activation(T.w0[:, a:a + wa], T.w0[:, PRE:PRE + wa], ACT.Copy))
     for Q, row in ((SY, OWN), (A, OWN + 1)):
         Q.wait_ge(S.v, f1)
         Q.wait_ge(S.a, fa0)
@@ -156,43 +167,42 @@ def rank_program(g, core, T, topo):
     na[1] = fa0
     loads = {d: 32 for d in IMPORTS}
     loads[0] = 48
+
     f2 = vec(lambda: V.memset(T.w1[:, 0:1024], 0.0))
     A.wait_ge(S.v, f2)
-    for a in (1024, 2048):
-        fa1 = act(lambda: A.activation(T.w1[:, a:a + 1024], T.w1[:, 0:1024], ACT.Copy))
+    for a in range(1024, FILL1[0], 512):
+        act(lambda: A.activation(T.w1[:, a:a + 512], T.w1[:, 0:512], ACT.Copy))
+    vec(lambda: V.memset(T.gt[:, 0:16], 0.0))
+    vec(lambda: V.memset(T.gt[:, 528:544], 0.0))
 
+    rows = sorted(set(w[1] for w in WIN.values()))
     V.wait_ge(S.gi, 3)
     vec(lambda: ts(T.k0[:, 0:1], T.pid[:, 0:1], 4, 1, op.arith_shift_right, op.bitwise_and))
     n = vec(lambda: ts(T.k0[:, 1:2], T.pid[:, 1:2], 255, None, op.bitwise_and))
-    vec(lambda: V.memset(T.gt[:, 0:16], 0.0))
-    vec(lambda: V.memset(T.gt[:, 528:544], 0.0))
     n = vec(lambda: V.tensor_copy(T.k1[:, 0:1], T.k0[:, 1:2]), n)
     n = vec(lambda: ts(T.k1[:, 1:2], T.k0[:, 0:1], 528.0, T.k1[:, 0:1], op.mult, op.add), n)
-    rows = sorted(set(w[1] for w in WIN.values()))
     for i, rho in enumerate(rows):
         vec(lambda: ts(T.pick[:, 4 * i:4 * i + 4], T.pat[:], T.k1[:, 1:2], float(rho), op.add, op.add), n)
     V.wait_ge(S.fac, 16)
     vec(lambda: ts(T.fs0[:], T.fown[:], 1.0 / 16, None, op.mult))
     V.wait_ge(S.ray, 64)
     n = vec(lambda: ts(T.hist[:, 0:64], T.raw[:, 0:64], 8.0, None, op.mult))
-    vec(lambda: V.tensor_tensor(T.tw[:], T.raw[:, 0:64], T.raw[:, 64:128], op.add))
+    m = vec(lambda: V.tensor_tensor(T.tw[:], T.raw[:, 0:64], T.raw[:, 64:128], op.add))
+    vec(lambda: ts(T.pre[:], T.tw[:], 8.0, -BIAS, op.mult, op.add), m)
+    twdone = [0]
 
     def slot(k, a=0, b=64):
         return T.hist[:, 64 * k + a:64 * k + b]
 
-    def cells(k, h, after):
+    def cells(k, j, after, stepping=True):
         vec(lambda: ts(T.cx[:], slot(k, 0, 32), 7, 127, op.arith_shift_right, op.bitwise_and), after)
         n = vec(lambda: ts(T.cy[:], slot(k, 32, 64), 63 * 128, None, op.bitwise_and))
-        if 0 < h < 7:
-            vec(lambda: ts(T.tw[:], slot(k), 2.0, -BIAS, op.mult, op.add))
-        n = vec(lambda: V.tensor_tensor(T.cell[:], T.cx[:], T.cy[:], op.add), n)
-        if h == 0:
-            vec(lambda: ts(T.pre[:], T.tw[:], 8.0, -BIAS, op.mult, op.add))
-        return vec(lambda: V.tensor_copy(T.ixl[:, 32 * h:32 * h + 32], T.cell[:]), n)
+        if stepping:
+            twdone[0] = vec(lambda: ts(T.tw[:], slot(k), 2.0, -BIAS, op.mult, op.add))
+        return vec(lambda: V.tensor_tensor(T.ixl[:, 32 * j:32 * j + 32], T.cx[:], T.cy[:], op.add), n)
 
     ready = {}
-    ixdone = {0: cells(0, 0, n)}
-
+    ixdone = {0: cells(0, 0, n, False)}
     vseen, aseen = set(), set()
 
     def gather_ready(Q, seen, h):
@@ -203,20 +213,22 @@ def rank_program(g, core, T, topo):
             if Q is A:
                 A.wait_ge(S.v, ixdone[h])
             return T.ixl
-        Q.wait_ge(S["ix%d" % h], cnt(O[h] - h, "ix%d" % h))
+        Q.wait_ge(S["ix%d" % h], cnt(made(h) - h, "ix%d" % h))
         return T.ixr
 
     gdone = {}
 
-    def e_act(h):
+    def e_act(h, a=0, b=32):
         buf = gather_ready(A, aseen, h)
-        return act(lambda: A.activation(T.gs[:, 512 * h:512 * h + 512],
-                                        T.ly[:].indirect(buf[:, 32 * h:32 * h + 32]), ACT.Copy))
+        n = act(lambda: A.activation(T.gs[:, 512 * h + 16 * a:512 * h + 16 * b],
+                                     T.ly[:].indirect(buf[:, 32 * h + a:32 * h + b]), ACT.Copy))
+        gdone.setdefault(h, []).append((S.a, n))
 
-    def e_vec(h):
+    def e_vec(h, a=0, b=32):
         buf = gather_ready(V, vseen, h)
-        return vec(lambda: V.tensor_copy(T.gs[:, 512 * h:512 * h + 512],
-                                         T.ly[:].indirect(buf[:, 32 * h:32 * h + 32])), ixdone.get(h, 0))
+        n = vec(lambda: V.tensor_copy(T.gs[:, 512 * h + 16 * a:512 * h + 16 * b],
+                                      T.ly[:].indirect(buf[:, 32 * h + a:32 * h + b])), ixdone.get(h, 0))
+        gdone.setdefault(h, []).append((S.v, n))
 
     cur = 0
     hops = {}
@@ -228,45 +240,52 @@ def rank_program(g, core, T, topo):
             V.wait_ge(S["st%d" % (h - 1)], cnt(O[h - 1] - O[h]))
             cur += 2
             ixdone[h] = cells(cur, h, pv)
-            ready["ix%d" % h] = [(S.v, ixdone[h])]
+            if h not in EARLY:
+                ready["ix%d" % h] = [(S.v, ixdone[h])]
+        fsc = T.fs0[:] if d == 0 else T.fs[:, d:d + 1]
+        ix = T.ixl
+
+        def pre(a, b):
+            if h > 0:
+                vec(lambda: V.tensor_tensor(T.pre[:, a:b], T.tw[:, a:b], slot(cur - 1, a, b), op.subtract),
+                    twdone[0])
+
+        pre(0, 32)
         for dd, (w2, _, gt) in WIN.items():
             if w2 == w and (gt is None or gt < h):
                 for Q, seen in ((V, vseen), (A, aseen)):
                     if ("w", dd) not in seen:
                         Q.wait_ge(S["wl%d" % dd], loads[dd])
                         seen.add(("w", dd))
-        fsc = T.fs0[:] if d == 0 else T.fs[:, d:d + 1]
-        ix = T.ixl
-
-        def pre(a, b):
-            if h > 0:
-                vec(lambda: V.tensor_tensor(T.pre[:, a:b], T.tw[:, a:b], slot(cur - 1, a, b), op.subtract))
-
-        pre(0, 32)
-        gv = vec(lambda: ts(T.gt[:, 16:16 + 16 * SPLIT], W[w][:].indirect(ix[:, 32 * h:32 * h + SPLIT]), fsc, RB,
+        c = 16 * SPLIT
+        gv = vec(lambda: ts(T.gt[:, 16:16 + c], W[w][:].indirect(ix[:, 32 * h:32 * h + SPLIT]), fsc, RB,
                             op.mult, op.add), ixdone[h])
         A.wait_ge(S.v, ixdone[h])
-        ga = act(lambda: A.activation(T.gt[:, 16 + 16 * SPLIT:528],
-                                      W[w][:].indirect(ix[:, 32 * h + SPLIT:32 * h + 32]),
+        ga = act(lambda: A.activation(T.gt[:, 16 + c:528], W[w][:].indirect(ix[:, 32 * h + SPLIT:32 * h + 32]),
                                       ACT.Identity, bias=RB, scale=fsc))
         pre(32, 64)
         gate[h] = (gv, ga)
+        vec(lambda: V.transpose(T.tt[:, 0:c], T.gt[:, 16:16 + c]), gv)
+        vec(lambda: V.transpose(T.tt[:, 512:512 + c], T.gt[:, 0:c]))
         V.wait_ge(S.a, ga)
-        vec(lambda: V.transpose(T.tt[:, 0:512], T.gt[:, 16:528]), gv)
-        n = vec(lambda: V.transpose(T.tt[:, 512:1056], T.gt[:, 0:544]))
+        vec(lambda: V.transpose(T.tt[:, c:512], T.gt[:, 16 + c:528]))
+        n = vec(lambda: V.transpose(T.tt[:, 512 + c:1056], T.gt[:, c:544]))
         i = rows.index(rho)
         pv = vec(lambda: V.tensor_tensor(slot(cur + 1), T.tt[:].indirect(T.pick[:, 4 * i:4 * i + 4]), T.pre[:],
                                          op.add), n)
         cur += 1
         if O[h + 1] == O[h]:
-            ixdone[h + 1] = cells(cur, h + 1, pv)
+            ixdone[h + 1] = cells(cur, h + 1, pv, h < 6)
             ready["ix%d" % (h + 1)] = [(S.v, ixdone[h + 1])]
         else:
             ready["st%d" % h] = [(S.v, pv)]
             hops[h] = cur
+            if h + 1 in EARLY:
+                pv = cells(cur, 8, pv, False)
+                ready["ix%d" % (h + 1)] = [(S.v, pv)]
         if h == 0:
-            f3 = vec(lambda: V.memset(T.w1[:, 5120:8192], 0.0))
-            for a in (3072, 4096):
+            f3 = vec(lambda: V.memset(T.w1[:, FILL1[1]:C], 0.0))
+            for a in range(FILL1[0], FILL1[1], 1024):
                 fa1 = act(lambda: A.activation(T.w1[:, a:a + 1024], T.w1[:, 0:1024], ACT.Copy))
             V.wait_ge(S.fa, nfa)
             lo, hi = min(IMPORTS), max(IMPORTS) + 1
@@ -275,9 +294,12 @@ def rank_program(g, core, T, topo):
             V.wait_ge(S.gd, 1)
             idn = vec(lambda: ts(T.ident[:], T.dif[:], 0.0, None, op.is_equal))
         for e in ACT_E.get(h, []):
-            gdone[e] = [(S.a, e_act(e))]
+            e_act(e)
         for e in DVE_E.get(h, []):
-            gdone[e] = [(S.v, e_vec(e))]
+            e_vec(e)
+    for e in LAST:
+        e_act(e, 16, 32)
+        e_vec(e, 0, 16)
     for h in range(1, 8):
         ready["G%d" % h] = gdone[h]
 
@@ -299,6 +321,8 @@ def rank_program(g, core, T, topo):
             load_lay(x)
         elif what == "win":
             reload(x)
+        elif what == "gate":
+            SY.wait_ge(S.v, gate[x][0])
         elif x == "wl0":
             SY.wait_ge(S.wl0, loads[0])
         else:
@@ -321,7 +345,8 @@ def rank_program(g, core, T, topo):
                 parts.append((T.hist[:, 64 * (k + 1):64 * (k + 3)], T.hist[:, 64 * (k - 1):64 * (k + 1)],
                               O[h + 1] - O[h], S[nm]))
             elif nm[:2] == "ix":
-                parts.append((T.ixr[:, 32 * h:32 * h + 32], T.ixl[:, 32 * h:32 * h + 32], h - O[h], S[nm]))
+                j = 8 if h in EARLY else h
+                parts.append((T.ixr[:, 32 * h:32 * h + 32], T.ixl[:, 32 * j:32 * j + 32], h - made(h), S[nm]))
             else:
                 parts.append((T.gl[:, 512 * h:512 * h + 512], T.gs[:, 512 * h:512 * h + 512], -h, S["ga%d" % h]))
         put(parts)
@@ -339,9 +364,11 @@ def rank_program(g, core, T, topo):
         mm = PE.matmul(T.ps[:], T.ident[:], src, j == 0, j == 6)
     mm.then_inc(S.pe, 1)
     V.wait_ge(S.pe, 1)
-    V.wait_ge(S.ga7, cnt(7, "G7"))
+    e = FINAL
+    V.wait_ge(S["ga%d" % e], cnt(e, "G%d" % e))
     for Q, a in ((SY, 0), (A, 256)):
-        n = vec(lambda: V.tensor_tensor(T.ys[:, a:a + 256], T.ps[:, a:a + 256], T.gl[:, 3584 + a:3840 + a], op.add))
+        b = 512 * e + a
+        n = vec(lambda: V.tensor_tensor(T.ys[:, a:a + 256], T.ps[:, a:a + 256], T.gl[:, b:b + 256], op.add))
         Q.wait_ge(S.v, n)
         Q.dma_start(T.y[:, a:a + 256], T.ys[:, a:a + 256]).then_inc(S.yd, 16)
     SY.wait_ge(S.yd, 32)

@@ -3,26 +3,28 @@ from concourse.mybir import AluOpType, ActivationFunctionType
 
 N = 8
 C = 8192
+OWN = 14
+STORES = 2
+ROW0 = 10
 O = [0, 4, 4, 4, 4, 7, 7, 7]
 EARLY = [5]
-OWN = 14
-WIN = {0: (0, OWN, None), 5: (0, 0, 0), 6: (1, 0, None), 7: (0, 2, 1)}
+WIN = {0: (0, OWN, None), 5: (0, 10, 0), 6: (1, 10, None), 7: (0, 12, 1)}
 IMPORTS = [5, 6, 7]
+LAST = ["G7", "G6", "G0"]
+FINAL = ["G6", "G6"]
+IDENT_AFTER = 4
 PRE = 1536
 FILL0 = (576, 3, 512)
-FILL1 = (2560, 4608)
-SY_HEAD = "fac stx px dx dy pre".split()
-ACT_HEAD = "sty py".split()
-ACT_E = {4: [1, 2], 5: [3], 6: [5]}
-DVE_E = {4: [4]}
-LAST = [7, 6, 0]
-FINAL = 6
-G_ORDER = "sl5 sl6 st0 sl7 id ix1+ix2 ix3 st4 ix5 G1+G4 G2 ix6 G3 G5 G7 G6".split()
+FILL1 = (2560, 4608, 8192)
+SY_HEAD = "fac sx px dx dy pre".split()
+ACT_HEAD = "sy py".split()
+ACT_E = {4: [(1, 0, 32), (2, 0, 32)], 5: [(3, 0, 32)], 6: [(5, 0, 32)]}
+DVE_E = {4: [(4, 0, 32)]}
+G_ORDER = "fa sx5+sy5 sx6+sy6 st0 sx7+sy7 id ix1+ix2 ix3 st4 ix5 G1+G4 G2 ix6 G3 G5 G7 G6".split()
 SYNC_ORDER = [("sem", "wl0"), ("lay", 1), ("win", 5), ("win", 6), ("lay", 2), ("win", 7), ("lay", 2), ("gate", 2),
               ("lay", 3)]
-PE_ORDER = [1, 4, 2, 3, 0, 5, 7]
-IDENT_AFTER = 4
-SPLIT = 12
+PE_ORDER = [1, 4, 2, 3, 5, 0, 7]
+SPLIT = 8
 BIAS = 1536.0
 RB = BIAS - 127.0 / 32.0
 
@@ -30,8 +32,8 @@ SCRATCH = {
     "ly": ("sbuf", [128, C], "bfloat16"),
     "w0": ("sbuf", [128, C], "bfloat16"),
     "w1": ("sbuf", [128, C], "bfloat16"),
-    "stage": ("dram", [128, 1024], "bfloat16"),
-    "land": ("dram", [3, 128, 1024], "bfloat16"),
+    "stage": ("dram", [2, 128, 512], "bfloat16"),
+    "land": ("dram", [2 * len(IMPORTS), 128, 512], "bfloat16"),
     "fown": ("sbuf", [128, 1], "int32"),
     "fl": ("sbuf", [128, 8], "int32"),
     "fs0": ("sbuf", [128, 1], "float32"),
@@ -44,10 +46,10 @@ SCRATCH = {
     "cy": ("sbuf", [128, 32], "int32"),
     "ixl": ("sbuf", [128, 32 * 9], "uint16"),
     "ixr": ("sbuf", [128, 32 * 8], "uint16"),
-    "gt": ("sbuf", [128, 544], "bfloat16"),
-    "tt": ("sbuf", [128, 1056], "bfloat16"),
+    "gt": ("sbuf", [128, 576], "bfloat16"),
+    "tt": ("sbuf", [128, 1088], "bfloat16"),
     "pid": ("sbuf", [128, 2], "int32"),
-    "pat": ("sbuf", [128, 4], "int32"),
+    "pat": ("sbuf", [128, 6], "int32"),
     "k0": ("sbuf", [128, 8], "int32"),
     "k1": ("sbuf", [128, 8], "float32"),
     "pick": ("sbuf", [128, 32], "uint16"),
@@ -56,11 +58,15 @@ SCRATCH = {
     "gs": ("sbuf", [128, 512 * 8], "bfloat16"),
     "gl": ("sbuf", [128, 512 * 8], "bfloat16"),
     "ys": ("sbuf", [128, 512], "float32"),
-    "ps": ("psum", [128, 512], "float32"),
+    "ps": ("psum", [128, 1024], "float32"),
 }
-SEMAPHORES = (["v", "a", "pe", "gi", "fac", "stg", "ray", "lay", "yd", "sent", "gf", "gd", "fa"]
-              + ["wl%d" % d for d in range(8)] + ["sa%d" % d for d in range(8)]
-              + ["st%d" % h for h in range(7)] + ["ix%d" % h for h in range(8)] + ["ga%d" % h for h in range(8)])
+WRITES = [nm for c in G_ORDER for nm in c.split("+") if nm not in ("id", "fill", "fa") and nm[0] != "@"]
+SEMAPHORES = (["v", "a", "pe", "gi", "fac", "sx", "sy", "rp", "rd", "lay", "yd", "sent", "gf", "gd", "fa"]
+              + ["wl%d" % d for d in WIN] + WRITES)
+
+
+def tile(nm):
+    return (int(nm[1]),) + {"": (0, 32), "a": (0, 16), "b": (16, 32)}[nm[2:]]
 
 
 def rank_program(g, core, T, topo):
@@ -72,12 +78,16 @@ def rank_program(g, core, T, topo):
     op = AluOpType
     ACT = ActivationFunctionType
     W = [T.w0, T.w1]
+    handed = [h for h in range(1, 7) if O[h] != O[h - 1]]
 
     def peer(d):
         return T.cores[(rank + d) % N]
 
-    def made(h):
-        return O[h - 1] if h in EARLY else O[h]
+    def reach(nm):
+        h = int(nm[1] if nm[0] == "G" else nm[2])
+        if nm[:2] == "ix":
+            return h - (O[h - 1] if h in EARLY else O[h])
+        return O[h + 1] - O[h] if nm[:2] == "st" else -h
 
     nv, na = [0, 0], [0, 0]
 
@@ -98,9 +108,9 @@ def rank_program(g, core, T, topo):
     ts = V.tensor_scalar
 
     first = {"fac": (T.fown[:], T.fac[:], S.fac),
-             "stx": (T.stage[0:64, :], T.lay[14::16, :], S.stg), "sty": (T.stage[64:128, :], T.lay[15::16, :], S.stg),
-             "px": (T.raw[:, 0:32], T.px[:], S.ray), "py": (T.raw[:, 32:64], T.py[:], S.ray),
-             "dx": (T.raw[:, 64:96], T.dx[:], S.ray), "dy": (T.raw[:, 96:128], T.dy[:], S.ray),
+             "sx": (T.stage[0], T.lay[14::16, :], S.sx), "sy": (T.stage[1], T.lay[15::16, :], S.sy),
+             "px": (T.raw[:, 0:32], T.px[:], S.rp), "py": (T.raw[:, 32:64], T.py[:], S.rp),
+             "dx": (T.raw[:, 64:96], T.dx[:], S.rd), "dy": (T.raw[:, 96:128], T.dy[:], S.rd),
              "pre": (T.w0[:, 0:PRE], T.lay[:, 0:PRE], S.wl0)}
     for Q, names in ((SY, SY_HEAD), (A, ACT_HEAD)):
         for nm in names:
@@ -113,45 +123,49 @@ def rank_program(g, core, T, topo):
             SY.dma_start(T.ly[k::8, :], T.lay[k::8, :]).then_inc(S.lay, 16)
             nlay[0] += 1
 
-    def deal(src, dst, j, n):
-        en = topo.engines(src, dst)
-        cuts = {1: [0, 4], 2: [0, 2, 4], 3: [0, 1, 2, 4]}[n]
-        return en[cuts[j] * len(en) // 4:cuts[j + 1] * len(en) // 4]
-
     place = {nm: (j, len(c.split("+"))) for c in G_ORDER for j, nm in enumerate(c.split("+"))}
 
-    def cnt(d, name=None):
-        return len(deal(peer(d), core, *place.get(name, (0, 1))))
+    def deal(src, dst, nm):
+        j, n = place[nm]
+        en = topo.engines(src, dst)
+        cuts = {1: [0, 4], 2: [0, 2, 4], 3: [0, 1, 2, 4], 4: [0, 1, 2, 3, 4]}[n]
+        return en[cuts[j] * len(en) // 4:cuts[j + 1] * len(en) // 4]
+
+    def landed(Q, nm):
+        Q.wait_ge(S[nm], len(deal(peer(-reach(nm)), core, nm)))
 
     sent = [0]
 
     def put(parts):
         trs = []
-        for j, (out, in_, d, rsem) in enumerate(parts):
-            en = deal(core, peer(d), j, len(parts))
-            rid, pid, _ = topo.addr(peer(d))
+        for nm, out, in_ in parts:
+            dst = peer(reach(nm))
+            en = deal(core, dst, nm)
+            rid, pid, _ = topo.addr(dst)
             sent[0] += len(en)
             if len(parts) == 1:
-                g.remote_dma(out, in_, rsem, S.sent, pid, rid, topo.mask(core, peer(d)))
+                g.remote_dma(out, in_, S[nm], S.sent, pid, rid, topo.mask(core, dst))
                 return
             trs.append(RemoteDMATransfer(dst_ids=[DstId(rid=rid, pnc=pid)], dma_engine_mask=sum(1 << e for e in en),
-                                         remote_sem=rsem, srcs=[in_], dsts=[out]))
+                                         remote_sem=S[nm], srcs=[in_], dsts=[out]))
         g.remote_dma_fused(trs, local_sem=S.sent)
+
+    def factors():
+        g.wait_ge(S.fac, 16)
+        m0 = topo.mask(core, peer(-IMPORTS[0]))
+        ids = [topo.addr(peer(-d)) for d in IMPORTS]
+        g.remote_dma_fused([RemoteDMATransfer(dst_ids=[DstId(rid=i[0], pnc=i[1]) for i in ids], dma_engine_mask=m0,
+                                              remote_sem=S.fa, srcs=[T.fown[:]],
+                                              dsts=[T.fl[:, d:d + 1] for d in IMPORTS])], local_sem=S.sent)
+        sent[0] += len(topo.engines(core, peer(-IMPORTS[0])))
+
+    nfa = sum(len(topo.engines(peer(d), peer(d - IMPORTS[0]))) for d in IMPORTS)
 
     wa, nA, wg = FILL0
     g.iota(T.w0[:, C - wg:C], [[0, wg]], 0, 0, allow_small_or_imprecise_dtypes=True).then_inc(S.gf, 1)
     g.iota(T.pid[:, 0:1], [[1, 1]], 0, 17).then_inc(S.gi, 1)
     g.iota(T.pid[:, 1:2], [[1, 1]], 0, 16).then_inc(S.gi, 1)
-    g.iota(T.pat[:], [[1, 2], [256, 2]], 0, 0).then_inc(S.gi, 1)
-    g.wait_ge(S.fac, 16)
-    m0 = topo.mask(core, peer(-IMPORTS[0]))
-    ids = [topo.addr(peer(-d)) for d in IMPORTS]
-    g.remote_dma_fused([RemoteDMATransfer(dst_ids=[DstId(rid=i[0], pnc=i[1]) for i in ids], dma_engine_mask=m0,
-                                          remote_sem=S.fa, srcs=[T.fown[:]],
-                                          dsts=[T.fl[:, d:d + 1] for d in IMPORTS])], local_sem=S.sent)
-    sent[0] += len(topo.engines(core, peer(-IMPORTS[0])))
-    nfa = sum(len(topo.engines(peer(d), peer(d - IMPORTS[0]))) for d in IMPORTS)
-    g.wait_ge(S.stg, 32)
+    g.iota(T.pat[:], [[2, 3], [1, 2]], ROW0, 0).then_inc(S.gi, 1)
 
     va = C - wg - nA * wa
     f0 = vec(lambda: V.memset(T.w0[:, PRE:PRE + wa], 0.0))
@@ -160,9 +174,9 @@ def rank_program(g, core, T, topo):
     for a in range(va, C - wg, wa):
         fa0 = act(lambda: A.activation(T.w0[:, a:a + wa], T.w0[:, PRE:PRE + wa], ACT.Copy))
     for Q, row in ((SY, OWN), (A, OWN + 1)):
-        Q.wait_ge(S.v, f1)
-        Q.wait_ge(S.a, fa0)
         Q.wait_ge(S.gf, 1)
+        Q.wait_ge(S.a, fa0)
+        Q.wait_ge(S.v, f1)
         Q.dma_start(T.w0[row::16, PRE:], T.lay[row::16, PRE:]).then_inc(S.wl0, 16)
     na[1] = fa0
     loads = {d: 32 for d in IMPORTS}
@@ -172,149 +186,174 @@ def rank_program(g, core, T, topo):
     A.wait_ge(S.v, f2)
     for a in range(1024, FILL1[0], 512):
         act(lambda: A.activation(T.w1[:, a:a + 512], T.w1[:, 0:512], ACT.Copy))
-    vec(lambda: V.memset(T.gt[:, 0:16], 0.0))
-    vec(lambda: V.memset(T.gt[:, 528:544], 0.0))
 
-    rows = sorted(set(w[1] for w in WIN.values()))
     V.wait_ge(S.gi, 3)
     vec(lambda: ts(T.k0[:, 0:1], T.pid[:, 0:1], 4, 1, op.arith_shift_right, op.bitwise_and))
     n = vec(lambda: ts(T.k0[:, 1:2], T.pid[:, 1:2], 255, None, op.bitwise_and))
-    n = vec(lambda: V.tensor_copy(T.k1[:, 0:1], T.k0[:, 1:2]), n)
-    n = vec(lambda: ts(T.k1[:, 1:2], T.k0[:, 0:1], 528.0, T.k1[:, 0:1], op.mult, op.add), n)
-    for i, rho in enumerate(rows):
-        vec(lambda: ts(T.pick[:, 4 * i:4 * i + 4], T.pat[:], T.k1[:, 1:2], float(rho), op.add, op.add), n)
+    for a, b in ((0, 16), (272, 304), (560, 576)):
+        vec(lambda: V.memset(T.gt[:, a:b], 0.0))
+    vec(lambda: ts(T.k1[:, 0:1], T.k0[:, 0:1], 272.0, None, op.mult), n)
+    n = vec(lambda: V.tensor_copy(T.k1[:, 1:2], T.k0[:, 1:2]))
     V.wait_ge(S.fac, 16)
     vec(lambda: ts(T.fs0[:], T.fown[:], 1.0 / 16, None, op.mult))
-    V.wait_ge(S.ray, 64)
-    n = vec(lambda: ts(T.hist[:, 0:64], T.raw[:, 0:64], 8.0, None, op.mult))
-    m = vec(lambda: V.tensor_tensor(T.tw[:], T.raw[:, 0:64], T.raw[:, 64:128], op.add))
-    vec(lambda: ts(T.pre[:], T.tw[:], 8.0, -BIAS, op.mult, op.add), m)
-    twdone = [0]
+    V.wait_ge(S.rp, 32)
+    quarters = [(32 * u + 16 * s, 32 * s + 16 * u) for u in range(2) for s in range(2)]
+    for a, b in quarters:
+        p0 = vec(lambda: ts(T.hist[:, a:a + 16], T.raw[:, b:b + 16], 8.0, None, op.mult))
+    vec(lambda: ts(T.pick[:, 0:6], T.pat[:], T.k1[:, 0:1], T.k1[:, 1:2], op.add, op.add), n)
 
     def slot(k, a=0, b=64):
         return T.hist[:, 64 * k + a:64 * k + b]
 
+    def lst(buf, j, a=0, b=32):
+        return buf[:, 32 * j + a:32 * j + b]
+
+    twdone = [0, 0]
+
+    def fields(k, u, after):
+        vec(lambda: ts(T.cx[:, 16 * u:16 * u + 16], slot(k, 32 * u, 32 * u + 16), 7, 127,
+                       op.arith_shift_right, op.bitwise_and), after)
+        return vec(lambda: ts(T.cy[:, 16 * u:16 * u + 16], slot(k, 32 * u + 16, 32 * u + 32), 63 * 128, None,
+                              op.bitwise_and))
+
+    def twice(k, u):
+        twdone[u] = vec(lambda: ts(T.tw[:, 32 * u:32 * u + 32], slot(k, 32 * u, 32 * u + 32), 2.0, -BIAS,
+                                   op.mult, op.add))
+
+    def ahead(k, u):
+        vec(lambda: V.tensor_tensor(T.pre[:, 32 * u:32 * u + 32], T.tw[:, 32 * u:32 * u + 32],
+                                    slot(k - 1, 32 * u, 32 * u + 32), op.subtract), twdone[u])
+
     def cells(k, j, after, stepping=True):
-        vec(lambda: ts(T.cx[:], slot(k, 0, 32), 7, 127, op.arith_shift_right, op.bitwise_and), after)
-        n = vec(lambda: ts(T.cy[:], slot(k, 32, 64), 63 * 128, None, op.bitwise_and))
+        def join(u, n):
+            return vec(lambda: V.tensor_tensor(lst(T.ixl, j, 16 * u, 16 * u + 16), T.cx[:, 16 * u:16 * u + 16],
+                                               T.cy[:, 16 * u:16 * u + 16], op.add), n)
+        n0 = fields(k, 0, after[0])
         if stepping:
-            twdone[0] = vec(lambda: ts(T.tw[:], slot(k), 2.0, -BIAS, op.mult, op.add))
-        return vec(lambda: V.tensor_tensor(T.ixl[:, 32 * j:32 * j + 32], T.cx[:], T.cy[:], op.add), n)
+            twice(k, 0)
+        n1 = fields(k, 1, after[1])
+        m0 = join(0, n0)
+        if stepping:
+            twice(k, 1)
+            ahead(k, 0)
+        return m0, join(1, n1)
 
-    ready = {}
-    ixdone = {0: cells(0, 0, n, False)}
-    vseen, aseen = set(), set()
+    halves = {0: cells(0, 0, (p0, p0), False)}
+    made = {0: halves[0][1]}
+    V.wait_ge(S.rd, 32)
+    for a, b in quarters:
+        n = vec(lambda: V.tensor_tensor(T.tw[:, a:a + 16], T.raw[:, b:b + 16], T.raw[:, 64 + b:80 + b], op.add))
+    vec(lambda: ts(T.pre[:], T.tw[:], 8.0, -BIAS, op.mult, op.add), n)
 
-    def gather_ready(Q, seen, h):
-        if "lay" not in seen:
-            Q.wait_ge(S.lay, 128)
-            seen.add("lay")
+    ready = {"sx": [(S.sx, 16)], "sy": [(S.sy, 16)]}
+    seen = set()
+
+    def once(Q, key, fn):
+        if (Q is V, key) not in seen:
+            seen.add((Q is V, key))
+            fn()
+
+    def gather(Q, nm, a, b):
+        h = int(nm[1])
+        once(Q, "lay", lambda: Q.wait_ge(S.lay, 128))
         if O[h] == h:
             if Q is A:
-                A.wait_ge(S.v, ixdone[h])
-            return T.ixl
-        Q.wait_ge(S["ix%d" % h], cnt(made(h) - h, "ix%d" % h))
-        return T.ixr
-
-    gdone = {}
-
-    def e_act(h, a=0, b=32):
-        buf = gather_ready(A, aseen, h)
-        n = act(lambda: A.activation(T.gs[:, 512 * h + 16 * a:512 * h + 16 * b],
-                                     T.ly[:].indirect(buf[:, 32 * h + a:32 * h + b]), ACT.Copy))
-        gdone.setdefault(h, []).append((S.a, n))
-
-    def e_vec(h, a=0, b=32):
-        buf = gather_ready(V, vseen, h)
-        n = vec(lambda: V.tensor_copy(T.gs[:, 512 * h + 16 * a:512 * h + 16 * b],
-                                      T.ly[:].indirect(buf[:, 32 * h + a:32 * h + b])), ixdone.get(h, 0))
-        gdone.setdefault(h, []).append((S.v, n))
+                A.wait_ge(S.v, made[h])
+            src = T.ly[:].indirect(lst(T.ixl, h, a, b))
+        else:
+            once(Q, h, lambda: landed(Q, "ix%d" % h))
+            src = T.ly[:].indirect(lst(T.ixr, h, a, b))
+        out = T.gs[:, 512 * h + 16 * a:512 * h + 16 * b]
+        if Q is A:
+            done = (S.a, act(lambda: A.activation(out, src, ACT.Copy)))
+        else:
+            done = (S.v, vec(lambda: V.tensor_copy(out, src), made.get(h, 0)))
+        ready.setdefault(nm, []).append(done)
 
     cur = 0
     hops = {}
     gate = {}
+    c = 16 * SPLIT
     for h in range(7):
         d = (h - O[h]) % N
         w, rho, _ = WIN[d]
-        if h > 0 and O[h] != O[h - 1]:
-            V.wait_ge(S["st%d" % (h - 1)], cnt(O[h - 1] - O[h]))
+        if h in handed:
+            landed(V, "st%d" % (h - 1))
             cur += 2
-            ixdone[h] = cells(cur, h, pv)
+            halves[h] = cells(cur, h, (last, last))
+            made[h] = halves[h][1]
             if h not in EARLY:
-                ready["ix%d" % h] = [(S.v, ixdone[h])]
+                ready["ix%d" % h] = [(S.v, made[h])]
+        for Q in (V, A):
+            for dd, (w2, _, gt) in WIN.items():
+                if w2 == w and (gt is None or gt < h):
+                    once(Q, "w%d" % dd, lambda: Q.wait_ge(S["wl%d" % dd], loads[dd]))
         fsc = T.fs0[:] if d == 0 else T.fs[:, d:d + 1]
-        ix = T.ixl
-
-        def pre(a, b):
-            if h > 0:
-                vec(lambda: V.tensor_tensor(T.pre[:, a:b], T.tw[:, a:b], slot(cur - 1, a, b), op.subtract),
-                    twdone[0])
-
-        pre(0, 32)
-        for dd, (w2, _, gt) in WIN.items():
-            if w2 == w and (gt is None or gt < h):
-                for Q, seen in ((V, vseen), (A, aseen)):
-                    if ("w", dd) not in seen:
-                        Q.wait_ge(S["wl%d" % dd], loads[dd])
-                        seen.add(("w", dd))
-        c = 16 * SPLIT
-        gv = vec(lambda: ts(T.gt[:, 16:16 + c], W[w][:].indirect(ix[:, 32 * h:32 * h + SPLIT]), fsc, RB,
-                            op.mult, op.add), ixdone[h])
-        A.wait_ge(S.v, ixdone[h])
-        ga = act(lambda: A.activation(T.gt[:, 16 + c:528], W[w][:].indirect(ix[:, 32 * h + SPLIT:32 * h + 32]),
-                                      ACT.Identity, bias=RB, scale=fsc))
-        pre(32, 64)
-        gate[h] = (gv, ga)
-        vec(lambda: V.transpose(T.tt[:, 0:c], T.gt[:, 16:16 + c]), gv)
-        vec(lambda: V.transpose(T.tt[:, 512:512 + c], T.gt[:, 0:c]))
-        V.wait_ge(S.a, ga)
-        vec(lambda: V.transpose(T.tt[:, c:512], T.gt[:, 16 + c:528]))
-        n = vec(lambda: V.transpose(T.tt[:, 512 + c:1056], T.gt[:, c:544]))
-        i = rows.index(rho)
-        pv = vec(lambda: V.tensor_tensor(slot(cur + 1), T.tt[:].indirect(T.pick[:, 4 * i:4 * i + 4]), T.pre[:],
-                                         op.add), n)
+        gv, ga, turned, picked = {}, {}, {}, {}
+        for u in range(2):
+            a = 288 * u + 16
+            if u == 1 and h > 0:
+                ahead(cur, 1)
+            gv[u] = vec(lambda: ts(T.gt[:, a:a + c], W[w][:].indirect(lst(T.ixl, h, 16 * u, 16 * u + SPLIT)), fsc, RB,
+                                   op.mult, op.add), halves[h][u])
+            A.wait_ge(S.v, halves[h][u])
+            ga[u] = act(lambda: A.activation(T.gt[:, a + c:a + 256],
+                                             W[w][:].indirect(lst(T.ixl, h, 16 * u + SPLIT, 16 * u + 16)),
+                                             ACT.Identity, bias=RB, scale=fsc))
+        gate[h] = (gv[1], ga[1])
+        for u in range(2):
+            V.wait_ge(S.a, ga[u])
+            vec(lambda: V.transpose(T.tt[:, 544 * u + 256:544 * u + 544], T.gt[:, 288 * u:288 * u + 288]), gv[u])
+            turned[u] = vec(lambda: V.transpose(T.tt[:, 544 * u:544 * u + 256], T.gt[:, 288 * u + 16:288 * u + 272]))
+        i = (rho - ROW0) // 2
+        for u in range(2):
+            picked[u] = vec(lambda: V.tensor_tensor(
+                slot(cur + 1, 32 * u, 32 * u + 32), T.tt[:, 544 * u:544 * u + 544].indirect(T.pick[:, 2 * i:2 * i + 2]),
+                T.pre[:, 32 * u:32 * u + 32], op.add), turned[u])
+        last = picked[1]
         cur += 1
-        if O[h + 1] == O[h]:
-            ixdone[h + 1] = cells(cur, h + 1, pv, h < 6)
-            ready["ix%d" % (h + 1)] = [(S.v, ixdone[h + 1])]
-        else:
-            ready["st%d" % h] = [(S.v, pv)]
+        if h + 1 in handed:
+            ready["st%d" % h] = [(S.v, last)]
             hops[h] = cur
             if h + 1 in EARLY:
-                pv = cells(cur, 8, pv, False)
-                ready["ix%d" % (h + 1)] = [(S.v, pv)]
+                last = cells(cur, 8, picked, False)[1]
+                ready["ix%d" % (h + 1)] = [(S.v, last)]
+        else:
+            halves[h + 1] = cells(cur, h + 1, picked, h < 6)
+            made[h + 1] = halves[h + 1][1]
+            ready["ix%d" % (h + 1)] = [(S.v, made[h + 1])]
         if h == 0:
-            f3 = vec(lambda: V.memset(T.w1[:, FILL1[1]:C], 0.0))
+            f3 = vec(lambda: V.memset(T.w1[:, FILL1[1]:FILL1[2]], 0.0))
             for a in range(FILL1[0], FILL1[1], 1024):
-                fa1 = act(lambda: A.activation(T.w1[:, a:a + 1024], T.w1[:, 0:1024], ACT.Copy))
+                b = min(a + 1024, FILL1[1])
+                fa1 = act(lambda: A.activation(T.w1[:, a:b], T.w1[:, 0:b - a], ACT.Copy))
             V.wait_ge(S.fa, nfa)
             lo, hi = min(IMPORTS), max(IMPORTS) + 1
-            pv = vec(lambda: ts(T.fs[:, lo:hi], T.fl[:, lo:hi], 1.0 / 16, None, op.mult))
+            last = vec(lambda: ts(T.fs[:, lo:hi], T.fl[:, lo:hi], 1.0 / 16, None, op.mult))
         if h == IDENT_AFTER:
             V.wait_ge(S.gd, 1)
             idn = vec(lambda: ts(T.ident[:], T.dif[:], 0.0, None, op.is_equal))
-        for e in ACT_E.get(h, []):
-            e_act(e)
-        for e in DVE_E.get(h, []):
-            e_vec(e)
-    for e in LAST:
-        e_act(e, 16, 32)
-        e_vec(e, 0, 16)
-    for h in range(1, 8):
-        ready["G%d" % h] = gdone[h]
+        for e, a, b in ACT_E.get(h, []):
+            gather(A, "G%d" % e, a, b)
+        for e, a, b in DVE_E.get(h, []):
+            gather(V, "G%d" % e, a, b)
+    for nm in LAST:
+        _, a, b = tile(nm)
+        gather(A, nm, (a + b) // 2, b)
+        gather(V, nm, a, (a + b) // 2)
 
     def reload(d):
         w, rho, gt = WIN[d]
-        i = IMPORTS.index(d)
-        SY.wait_ge(S["sa%d" % d], cnt(d))
-        if w == 1:
-            SY.wait_ge(S.v, f3)
+        if gt is None:
+            SY.wait_ge(S.gf, 1 + G_ORDER.count("fill"))
             SY.wait_ge(S.a, fa1)
-        if gt is not None:
+            SY.wait_ge(S.v, f3)
+        else:
             SY.wait_ge(S.v, gate[gt][0])
             SY.wait_ge(S.a, gate[gt][1])
-        SY.dma_start(W[w][rho::16, :], T.land[i, 0:64, :]).then_inc(S["wl%d" % d], 16)
-        SY.dma_start(W[w][rho + 1::16, :], T.land[i, 64:128, :]).then_inc(S["wl%d" % d], 16)
+        for s, nm in enumerate(("sx%d" % d, "sy%d" % d)):
+            landed(SY, nm)
+            SY.dma_start(W[w][rho + s::16, :], T.land[2 * IMPORTS.index(d) + s]).then_inc(S["wl%d" % d], 16)
 
     for what, x in SYNC_ORDER:
         if what == "lay":
@@ -326,49 +365,68 @@ def rank_program(g, core, T, topo):
         elif x == "wl0":
             SY.wait_ge(S.wl0, loads[0])
         else:
-            h = int(x[-1])
-            SY.wait_ge(S[x], cnt(O[h] - O[h + 1]))
+            landed(SY, x)
 
     for name in G_ORDER:
         if name == "id":
             g.iota(T.dif[:], [[1, 128]], 0, -1).then_inc(S.gd, 1)
             continue
+        if name == "fa":
+            factors()
+            continue
+        if name[0] == "@":
+            landed(g, name[1:])
+            continue
+        if name == "fill":
+            g.iota(T.w1[:, FILL1[2]:C], [[0, C - FILL1[2]]], 0, 0,
+                   allow_small_or_imprecise_dtypes=True).then_inc(S.gf, 1)
+            continue
         parts = []
         for nm in name.split("+"):
-            for s, n in ready.get(nm, []):
+            kind = nm[:2]
+            for s, n in ready[kind if kind in ("sx", "sy") else nm]:
                 g.wait_ge(s, n)
-            h = int(nm[-1])
-            if nm[:2] == "sl":
-                parts.append((T.land[IMPORTS.index(h)], T.stage[:], -h, S["sa%d" % h]))
-            elif nm[:2] == "st":
-                k = hops[h]
-                parts.append((T.hist[:, 64 * (k + 1):64 * (k + 3)], T.hist[:, 64 * (k - 1):64 * (k + 1)],
-                              O[h + 1] - O[h], S[nm]))
-            elif nm[:2] == "ix":
-                j = 8 if h in EARLY else h
-                parts.append((T.ixr[:, 32 * h:32 * h + 32], T.ixl[:, 32 * j:32 * j + 32], h - made(h), S[nm]))
+            if nm[0] == "G":
+                h, a, b = tile(nm)
+                a, b = 512 * h + 16 * a, 512 * h + 16 * b
+                parts.append((nm, T.gl[:, a:b], T.gs[:, a:b]))
+                continue
+            h = int(nm[2])
+            if kind in ("sx", "sy"):
+                s = int(kind == "sy")
+                parts.append((nm, T.land[2 * IMPORTS.index(h) + s], T.stage[s]))
+            elif kind == "st":
+                parts.append((nm, slot(hops[h] + 1, 0, 128), slot(hops[h] - 1, 0, 128)))
             else:
-                parts.append((T.gl[:, 512 * h:512 * h + 512], T.gs[:, 512 * h:512 * h + 512], -h, S["ga%d" % h]))
+                parts.append((nm, lst(T.ixr, h), lst(T.ixl, 8 if h in EARLY else h)))
         put(parts)
     g.wait_ge(S.sent, sent[0])
 
     PE.wait_ge(S.v, idn)
     for j, h in enumerate(PE_ORDER):
         if h == 0:
-            for s, n in gdone[0]:
+            for s, n in ready["G0"]:
                 PE.wait_ge(s, n)
-            src = T.gs[:, 0:512]
+            src = T.gs
         else:
-            PE.wait_ge(S["ga%d" % h], cnt(h, "G%d" % h))
-            src = T.gl[:, 512 * h:512 * h + 512]
-        mm = PE.matmul(T.ps[:], T.ident[:], src, j == 0, j == 6)
-    mm.then_inc(S.pe, 1)
-    V.wait_ge(S.pe, 1)
-    e = FINAL
-    V.wait_ge(S["ga%d" % e], cnt(e, "G%d" % e))
-    for Q, a in ((SY, 0), (A, 256)):
-        b = 512 * e + a
-        n = vec(lambda: V.tensor_tensor(T.ys[:, a:a + 256], T.ps[:, a:a + 256], T.gl[:, b:b + 256], op.add))
-        Q.wait_ge(S.v, n)
-        Q.dma_start(T.y[:, a:a + 256], T.ys[:, a:a + 256]).then_inc(S.yd, 16)
-    SY.wait_ge(S.yd, 32)
+            landed(PE, "G%d" % h)
+            src = T.gl
+        for u in range(2):
+            a = 512 * h + 256 * u
+            mm = PE.matmul(T.ps[:, 512 * u:512 * u + 256], T.ident[:], src[:, a:a + 256], j == 0, j == 6)
+            if j == 6:
+                mm.then_inc(S.pe, 1)
+    k = 0
+    for u, nm in enumerate(FINAL):
+        h = int(nm[1])
+        V.wait_ge(S.pe, u + 1)
+        landed(V, nm)
+        for a in range(256 * u, 256 * u + 256, 512 // STORES):
+            b = a + 512 // STORES
+            n = vec(lambda: V.tensor_tensor(T.ys[:, a:b], T.ps[:, a + 256 * u:b + 256 * u],
+                                            T.gl[:, 512 * h + a:512 * h + b], op.add))
+            Q = (SY, A)[k % 2]
+            Q.wait_ge(S.v, n)
+            Q.dma_start(T.y[:, a:b], T.ys[:, a:b]).then_inc(S.yd, 16)
+            k += 1
+    SY.wait_ge(S.yd, 16 * STORES)

@@ -4,26 +4,26 @@ from concourse.mybir import AluOpType, ActivationFunctionType
 N = 8
 C = 8192
 OWN = 14
-STORES = 2
+STORES = 4
 ROW0 = 10
 O = [0, 4, 4, 4, 4, 7, 7, 7]
 EARLY = [5]
 WIN = {0: (0, OWN, None), 5: (0, 10, 0), 6: (1, 10, None), 7: (0, 12, 1)}
 IMPORTS = [5, 6, 7]
-LAST = ["G7", "G6", "G0"]
-FINAL = ["G6", "G6"]
-IDENT_AFTER = 4
-PRE = 1536
-FILL0 = (576, 3, 512)
-FILL1 = (2560, 4608, 8192)
+LAST = [("V", "G6", 24, 32), ("A", "G7a", 0, 16), ("V", "G7b", 16, 30), ("A", "G7b", 30, 32), ("V", "G0", 0, 16),
+        ("A", "G0", 16, 32)]
+FINAL = ["G7a", "G7b"]
+IDENT_IN = [2, 3]
+PRE = 1280
+FILL0 = (608, 3, 512)
+FILL1 = (2560, 4992, 7680)
 SY_HEAD = "fac sx px dx dy pre".split()
-ACT_HEAD = "sy py".split()
-ACT_E = {4: [(1, 0, 32), (2, 0, 32)], 5: [(3, 0, 32)], 6: [(5, 0, 32)]}
-DVE_E = {4: [(4, 0, 32)]}
-G_ORDER = "fa sx5+sy5 sx6+sy6 st0 sx7+sy7 id ix1+ix2 ix3 st4 ix5 G1+G4 G2 ix6 G3 G5 G7 G6".split()
-SYNC_ORDER = [("sem", "wl0"), ("lay", 1), ("win", 5), ("win", 6), ("lay", 2), ("win", 7), ("lay", 2), ("gate", 2),
-              ("lay", 3)]
-PE_ORDER = [1, 4, 2, 3, 5, 0, 7]
+ACT_HEAD = "py sy".split()
+ACT_E = {4: [(4, 28, 32), (1, 0, 32), (2, 0, 12)], 5: [(2, 12, 32), (3, 0, 32)], 6: [(5, 0, 32), (6, 0, 24)]}
+DVE_E = {4: [(4, 0, 28)]}
+G_ORDER = "fa sx5 sy5 sx6+sy6 fill st0 sx7+sy7 id ix1+ix2 ix3 sq4 st4 ix5 G1+G4 G2 ix6 G3 G5 G6 G7a G7b".split()
+SYNC_ORDER = [("win", 5), ("win", 6), ("lay", 2), ("win", 7), ("lay", 3), ("gate", 2), ("lay", 3)]
+PE_ORDER = [1, 4, 2, 3, 5, 0, 6]
 SPLIT = 8
 BIAS = 1536.0
 RB = BIAS - 127.0 / 32.0
@@ -36,10 +36,9 @@ SCRATCH = {
     "land": ("dram", [2 * len(IMPORTS), 128, 512], "bfloat16"),
     "fown": ("sbuf", [128, 1], "int32"),
     "fl": ("sbuf", [128, 8], "int32"),
-    "fs0": ("sbuf", [128, 1], "float32"),
     "fs": ("sbuf", [128, 8], "float32"),
     "raw": ("sbuf", [128, 128], "int32"),
-    "hist": ("sbuf", [128, 64 * 16], "int32"),
+    "hist": ("sbuf", [128, 64 * 24], "int32"),
     "pre": ("sbuf", [128, 64], "float32"),
     "tw": ("sbuf", [128, 64], "float32"),
     "cx": ("sbuf", [128, 32], "int32"),
@@ -58,11 +57,15 @@ SCRATCH = {
     "gs": ("sbuf", [128, 512 * 8], "bfloat16"),
     "gl": ("sbuf", [128, 512 * 8], "bfloat16"),
     "ys": ("sbuf", [128, 512], "float32"),
-    "ps": ("psum", [128, 1024], "float32"),
+    "ps": ("psum", [128, 512 * STORES], "float32"),
 }
 WRITES = [nm for c in G_ORDER for nm in c.split("+") if nm not in ("id", "fill", "fa") and nm[0] != "@"]
 SEMAPHORES = (["v", "a", "pe", "gi", "fac", "sx", "sy", "rp", "rd", "lay", "yd", "sent", "gf", "gd", "fa"]
               + ["wl%d" % d for d in WIN] + WRITES)
+
+
+def unit(h):
+    return 8 << (7 - h)
 
 
 def tile(nm):
@@ -87,7 +90,7 @@ def rank_program(g, core, T, topo):
         h = int(nm[1] if nm[0] == "G" else nm[2])
         if nm[:2] == "ix":
             return h - (O[h - 1] if h in EARLY else O[h])
-        return O[h + 1] - O[h] if nm[:2] == "st" else -h
+        return O[h + 1] - O[h] if nm[:2] in ("st", "sq") else -h
 
     nv, na = [0, 0], [0, 0]
 
@@ -185,7 +188,8 @@ def rank_program(g, core, T, topo):
     f2 = vec(lambda: V.memset(T.w1[:, 0:1024], 0.0))
     A.wait_ge(S.v, f2)
     for a in range(1024, FILL1[0], 512):
-        act(lambda: A.activation(T.w1[:, a:a + 512], T.w1[:, 0:512], ACT.Copy))
+        b = min(a + 512, FILL1[0])
+        act(lambda: A.activation(T.w1[:, a:b], T.w1[:, 0:b - a], ACT.Copy))
 
     V.wait_ge(S.gi, 3)
     vec(lambda: ts(T.k0[:, 0:1], T.pid[:, 0:1], 4, 1, op.arith_shift_right, op.bitwise_and))
@@ -195,11 +199,17 @@ def rank_program(g, core, T, topo):
     vec(lambda: ts(T.k1[:, 0:1], T.k0[:, 0:1], 272.0, None, op.mult), n)
     n = vec(lambda: V.tensor_copy(T.k1[:, 1:2], T.k0[:, 1:2]))
     V.wait_ge(S.fac, 16)
-    vec(lambda: ts(T.fs0[:], T.fown[:], 1.0 / 16, None, op.mult))
+
+    def factor(h):
+        d = (h - O[h]) % N
+        return vec(lambda: ts(T.fs[:, h:h + 1], T.fl[:, d:d + 1] if d else T.fown[:], unit(h + 1) / 128.0, None,
+                              op.mult))
+
+    factor(0)
     V.wait_ge(S.rp, 32)
     quarters = [(32 * u + 16 * s, 32 * s + 16 * u) for u in range(2) for s in range(2)]
     for a, b in quarters:
-        p0 = vec(lambda: ts(T.hist[:, a:a + 16], T.raw[:, b:b + 16], 8.0, None, op.mult))
+        p0 = vec(lambda: ts(T.hist[:, a:a + 16], T.raw[:, b:b + 16], float(unit(0)), None, op.mult))
     vec(lambda: ts(T.pick[:, 0:6], T.pat[:], T.k1[:, 0:1], T.k1[:, 1:2], op.add, op.add), n)
 
     def slot(k, a=0, b=64):
@@ -208,44 +218,44 @@ def rank_program(g, core, T, topo):
     def lst(buf, j, a=0, b=32):
         return buf[:, 32 * j + a:32 * j + b]
 
-    twdone = [0, 0]
+    ready = {"sx": [(S.sx, 16)], "sy": [(S.sy, 16)]}
 
-    def fields(k, u, after):
-        vec(lambda: ts(T.cx[:, 16 * u:16 * u + 16], slot(k, 32 * u, 32 * u + 16), 7, 127,
+    def fields(k, h, u, after):
+        vec(lambda: ts(T.cx[:, 16 * u:16 * u + 16], slot(k, 32 * u, 32 * u + 16), 14 - h, 127,
                        op.arith_shift_right, op.bitwise_and), after)
-        return vec(lambda: ts(T.cy[:, 16 * u:16 * u + 16], slot(k, 32 * u + 16, 32 * u + 32), 63 * 128, None,
-                              op.bitwise_and))
-
-    def twice(k, u):
-        twdone[u] = vec(lambda: ts(T.tw[:, 32 * u:32 * u + 32], slot(k, 32 * u, 32 * u + 32), 2.0, -BIAS,
-                                   op.mult, op.add))
+        return vec(lambda: ts(T.cy[:, 16 * u:16 * u + 16], slot(k, 32 * u + 16, 32 * u + 32), 7 - h, 63 * 128,
+                              op.arith_shift_right, op.bitwise_and))
 
     def ahead(k, u):
-        vec(lambda: V.tensor_tensor(T.pre[:, 32 * u:32 * u + 32], T.tw[:, 32 * u:32 * u + 32],
-                                    slot(k - 1, 32 * u, 32 * u + 32), op.subtract), twdone[u])
+        vec(lambda: V.tensor_tensor(T.pre[:, 32 * u:32 * u + 32], slot(k, 32 * u, 32 * u + 32),
+                                    slot(k - 1, 32 * u, 32 * u + 32), op.subtract))
 
-    def cells(k, j, after, stepping=True):
+    def behind(k, h):
+        n = vec(lambda: ts(slot(k + 1), slot(k), 0.25, BIAS * unit(h + 2) / 8, op.mult, op.add))
+        ready["sq%d" % h] = [(S.v, n)]
+
+    def cells(k, h, j, after, stepping=True):
         def join(u, n):
             return vec(lambda: V.tensor_tensor(lst(T.ixl, j, 16 * u, 16 * u + 16), T.cx[:, 16 * u:16 * u + 16],
                                                T.cy[:, 16 * u:16 * u + 16], op.add), n)
-        n0 = fields(k, 0, after[0])
+        n0 = fields(k, h, 0, after[0])
         if stepping:
-            twice(k, 0)
-        n1 = fields(k, 1, after[1])
+            ahead(k, 0)
+        n1 = fields(k, h, 1, after[1])
         m0 = join(0, n0)
         if stepping:
-            twice(k, 1)
-            ahead(k, 0)
+            ahead(k, 1)
+            if h < 6:
+                behind(k, h)
         return m0, join(1, n1)
 
-    halves = {0: cells(0, 0, (p0, p0), False)}
-    made = {0: halves[0][1]}
     V.wait_ge(S.rd, 32)
     for a, b in quarters:
         n = vec(lambda: V.tensor_tensor(T.tw[:, a:a + 16], T.raw[:, b:b + 16], T.raw[:, 64 + b:80 + b], op.add))
-    vec(lambda: ts(T.pre[:], T.tw[:], 8.0, -BIAS, op.mult, op.add), n)
+    halves = {0: cells(0, 0, 0, (p0, p0), False)}
+    made = {0: halves[0][1]}
+    vec(lambda: ts(T.pre[:], T.tw[:], float(unit(1)), -BIAS * unit(1) / 8, op.mult, op.add), n)
 
-    ready = {"sx": [(S.sx, 16)], "sy": [(S.sy, 16)]}
     seen = set()
 
     def once(Q, key, fn):
@@ -278,9 +288,11 @@ def rank_program(g, core, T, topo):
         d = (h - O[h]) % N
         w, rho, _ = WIN[d]
         if h in handed:
+            if "sq%d" % (h - 1) in WRITES:
+                landed(V, "sq%d" % (h - 1))
             landed(V, "st%d" % (h - 1))
             cur += 2
-            halves[h] = cells(cur, h, (last, last))
+            halves[h] = cells(cur, h, h, (last, last))
             made[h] = halves[h][1]
             if h not in EARLY:
                 ready["ix%d" % h] = [(S.v, made[h])]
@@ -288,18 +300,16 @@ def rank_program(g, core, T, topo):
             for dd, (w2, _, gt) in WIN.items():
                 if w2 == w and (gt is None or gt < h):
                     once(Q, "w%d" % dd, lambda: Q.wait_ge(S["wl%d" % dd], loads[dd]))
-        fsc = T.fs0[:] if d == 0 else T.fs[:, d:d + 1]
+        fsc, rb = T.fs[:, h:h + 1], RB * unit(h + 1) / 8
         gv, ga, turned, picked = {}, {}, {}, {}
         for u in range(2):
             a = 288 * u + 16
-            if u == 1 and h > 0:
-                ahead(cur, 1)
-            gv[u] = vec(lambda: ts(T.gt[:, a:a + c], W[w][:].indirect(lst(T.ixl, h, 16 * u, 16 * u + SPLIT)), fsc, RB,
+            gv[u] = vec(lambda: ts(T.gt[:, a:a + c], W[w][:].indirect(lst(T.ixl, h, 16 * u, 16 * u + SPLIT)), fsc, rb,
                                    op.mult, op.add), halves[h][u])
             A.wait_ge(S.v, halves[h][u])
             ga[u] = act(lambda: A.activation(T.gt[:, a + c:a + 256],
                                              W[w][:].indirect(lst(T.ixl, h, 16 * u + SPLIT, 16 * u + 16)),
-                                             ACT.Identity, bias=RB, scale=fsc))
+                                             ACT.Identity, bias=rb, scale=fsc))
         gate[h] = (gv[1], ga[1])
         for u in range(2):
             V.wait_ge(S.a, ga[u])
@@ -308,18 +318,26 @@ def rank_program(g, core, T, topo):
         i = (rho - ROW0) // 2
         for u in range(2):
             picked[u] = vec(lambda: V.tensor_tensor(
-                slot(cur + 1, 32 * u, 32 * u + 32), T.tt[:, 544 * u:544 * u + 544].indirect(T.pick[:, 2 * i:2 * i + 2]),
+                slot(cur + 2, 32 * u, 32 * u + 32), T.tt[:, 544 * u:544 * u + 544].indirect(T.pick[:, 2 * i:2 * i + 2]),
                 T.pre[:, 32 * u:32 * u + 32], op.add), turned[u])
+            if u == 0 and h == 0:
+                behind(0, 0)
+            elif u == 0 and h < 6:
+                factor(h + 1)
+                if h in IDENT_IN:
+                    a = 64 * IDENT_IN.index(h)
+                    once(V, "id", lambda: V.wait_ge(S.gd, 1))
+                    idn = vec(lambda: ts(T.ident[:, a:a + 64], T.dif[:, a:a + 64], 0.0, None, op.is_equal))
         last = picked[1]
-        cur += 1
+        cur += 2
         if h + 1 in handed:
             ready["st%d" % h] = [(S.v, last)]
             hops[h] = cur
             if h + 1 in EARLY:
-                last = cells(cur, 8, picked, False)[1]
+                last = cells(cur, h + 1, 8, picked, False)[1]
                 ready["ix%d" % (h + 1)] = [(S.v, last)]
         else:
-            halves[h + 1] = cells(cur, h + 1, picked, h < 6)
+            halves[h + 1] = cells(cur, h + 1, h + 1, picked, h < 6)
             made[h + 1] = halves[h + 1][1]
             ready["ix%d" % (h + 1)] = [(S.v, made[h + 1])]
         if h == 0:
@@ -328,19 +346,13 @@ def rank_program(g, core, T, topo):
                 b = min(a + 1024, FILL1[1])
                 fa1 = act(lambda: A.activation(T.w1[:, a:b], T.w1[:, 0:b - a], ACT.Copy))
             V.wait_ge(S.fa, nfa)
-            lo, hi = min(IMPORTS), max(IMPORTS) + 1
-            last = vec(lambda: ts(T.fs[:, lo:hi], T.fl[:, lo:hi], 1.0 / 16, None, op.mult))
-        if h == IDENT_AFTER:
-            V.wait_ge(S.gd, 1)
-            idn = vec(lambda: ts(T.ident[:], T.dif[:], 0.0, None, op.is_equal))
+            last = factor(1)
         for e, a, b in ACT_E.get(h, []):
             gather(A, "G%d" % e, a, b)
         for e, a, b in DVE_E.get(h, []):
             gather(V, "G%d" % e, a, b)
-    for nm in LAST:
-        _, a, b = tile(nm)
-        gather(A, nm, (a + b) // 2, b)
-        gather(V, nm, a, (a + b) // 2)
+    for q, nm, a, b in LAST:
+        gather(V if q == "V" else A, nm, a, b)
 
     def reload(d):
         w, rho, gt = WIN[d]
@@ -353,6 +365,8 @@ def rank_program(g, core, T, topo):
             SY.wait_ge(S.a, gate[gt][1])
         for s, nm in enumerate(("sx%d" % d, "sy%d" % d)):
             landed(SY, nm)
+            if s == 1 and "st%s" % gt in ready:
+                SY.wait_ge(*ready["st%d" % gt][0])
             SY.dma_start(W[w][rho + s::16, :], T.land[2 * IMPORTS.index(d) + s]).then_inc(S["wl%d" % d], 16)
 
     for what, x in SYNC_ORDER:
@@ -396,12 +410,16 @@ def rank_program(g, core, T, topo):
                 s = int(kind == "sy")
                 parts.append((nm, T.land[2 * IMPORTS.index(h) + s], T.stage[s]))
             elif kind == "st":
-                parts.append((nm, slot(hops[h] + 1, 0, 128), slot(hops[h] - 1, 0, 128)))
+                a = -64 * ("sq%d" % h not in WRITES)
+                parts.append((nm, slot(hops[h] + 2, a), slot(hops[h], a)))
+            elif kind == "sq":
+                parts.append((nm, slot(hops[h] + 1), slot(hops[h] - 1)))
             else:
                 parts.append((nm, lst(T.ixr, h), lst(T.ixl, 8 if h in EARLY else h)))
         put(parts)
     g.wait_ge(S.sent, sent[0])
 
+    wy = 512 // STORES
     PE.wait_ge(S.v, idn)
     for j, h in enumerate(PE_ORDER):
         if h == 0:
@@ -411,22 +429,19 @@ def rank_program(g, core, T, topo):
         else:
             landed(PE, "G%d" % h)
             src = T.gl
-        for u in range(2):
-            a = 512 * h + 256 * u
-            mm = PE.matmul(T.ps[:, 512 * u:512 * u + 256], T.ident[:], src[:, a:a + 256], j == 0, j == 6)
+        for u in range(STORES):
+            a = 512 * h + wy * u
+            mm = PE.matmul(T.ps[:, 512 * u:512 * u + wy], T.ident[:], src[:, a:a + wy], j == 0, j == 6)
             if j == 6:
                 mm.then_inc(S.pe, 1)
-    k = 0
-    for u, nm in enumerate(FINAL):
-        h = int(nm[1])
+    for u in range(STORES):
+        nm = FINAL[2 * u // STORES]
+        h, a, b = int(nm[1]), wy * u, wy * u + wy
         V.wait_ge(S.pe, u + 1)
         landed(V, nm)
-        for a in range(256 * u, 256 * u + 256, 512 // STORES):
-            b = a + 512 // STORES
-            n = vec(lambda: V.tensor_tensor(T.ys[:, a:b], T.ps[:, a + 256 * u:b + 256 * u],
-                                            T.gl[:, 512 * h + a:512 * h + b], op.add))
-            Q = (SY, A)[k % 2]
-            Q.wait_ge(S.v, n)
-            Q.dma_start(T.y[:, a:b], T.ys[:, a:b]).then_inc(S.yd, 16)
-            k += 1
+        n = vec(lambda: V.tensor_tensor(T.ys[:, a:b], T.ps[:, 512 * u:512 * u + wy],
+                                        T.gl[:, 512 * h + a:512 * h + b], op.add))
+        Q = (SY, A)[u % 2]
+        Q.wait_ge(S.v, n)
+        Q.dma_start(T.y[:, a:b], T.ys[:, a:b]).then_inc(S.yd, 16)
     SY.wait_ge(S.yd, 16 * STORES)

from concourse.bass import DstId, RemoteDMATransfer
from concourse.mybir import AluOpType, ActivationFunctionType

N = 8
C = 8192
OWN = 14
STORES = 4
ROW0 = 10
O = [0, 4, 4, 4, 4, 7, 7, 7]
EARLY = [5]
WIN = {0: (0, OWN, None), 5: (0, 10, 0), 6: (1, 10, None), 7: (0, 12, 1)}
IMPORTS = [5, 6, 7]
LAST = [("V", "G6", 24, 32), ("A", "G7a", 0, 16), ("V", "G7b", 16, 30), ("A", "G7b", 30, 32), ("V", "G0", 0, 16),
        ("A", "G0", 16, 32)]
FINAL = ["G7a", "G7b"]
IDENT_IN = [2, 3]
PRE = 1280
FILL0 = (608, 3, 512)
FILL1 = (2560, 4992, 7680)
SY_HEAD = "fac sx px dx dy pre".split()
ACT_HEAD = "py sy".split()
ACT_E = {4: [(4, 28, 32), (1, 0, 32), (2, 0, 12)], 5: [(2, 12, 32), (3, 0, 32)], 6: [(5, 0, 32), (6, 0, 24)]}
DVE_E = {4: [(4, 0, 28)]}
G_ORDER = "fa sx5 sy5 sx6+sy6 fill st0 sx7+sy7 id ix1+ix2 ix3 sq4 st4 ix5 G1+G4 G2 ix6 G3 G5 G6 G7a G7b".split()
SYNC_ORDER = [("win", 5), ("win", 6), ("lay", 2), ("win", 7), ("lay", 3), ("gate", 2), ("lay", 3)]
PE_ORDER = [1, 4, 2, 3, 5, 0, 6]
SPLIT = 8
BIAS = 1536.0
RB = BIAS - 127.0 / 32.0

SCRATCH = {
    "ly": ("sbuf", [128, C], "bfloat16"),
    "w0": ("sbuf", [128, C], "bfloat16"),
    "w1": ("sbuf", [128, C], "bfloat16"),
    "stage": ("dram", [2, 128, 512], "bfloat16"),
    "land": ("dram", [2 * len(IMPORTS), 128, 512], "bfloat16"),
    "fown": ("sbuf", [128, 1], "int32"),
    "fl": ("sbuf", [128, 8], "int32"),
    "fs": ("sbuf", [128, 8], "float32"),
    "raw": ("sbuf", [128, 128], "int32"),
    "hist": ("sbuf", [128, 64 * 24], "int32"),
    "pre": ("sbuf", [128, 64], "float32"),
    "tw": ("sbuf", [128, 64], "float32"),
    "cx": ("sbuf", [128, 32], "int32"),
    "cy": ("sbuf", [128, 32], "int32"),
    "ixl": ("sbuf", [128, 32 * 9], "uint16"),
    "ixr": ("sbuf", [128, 32 * 8], "uint16"),
    "gt": ("sbuf", [128, 576], "bfloat16"),
    "tt": ("sbuf", [128, 1088], "bfloat16"),
    "pid": ("sbuf", [128, 2], "int32"),
    "pat": ("sbuf", [128, 6], "int32"),
    "k0": ("sbuf", [128, 8], "int32"),
    "k1": ("sbuf", [128, 8], "float32"),
    "pick": ("sbuf", [128, 32], "uint16"),
    "dif": ("sbuf", [128, 128], "int32"),
    "ident": ("sbuf", [128, 128], "bfloat16"),
    "gs": ("sbuf", [128, 512 * 8], "bfloat16"),
    "gl": ("sbuf", [128, 512 * 8], "bfloat16"),
    "ys": ("sbuf", [128, 512], "float32"),
    "ps": ("psum", [128, 512 * STORES], "float32"),
}
WRITES = [nm for c in G_ORDER for nm in c.split("+") if nm not in ("id", "fill", "fa") and nm[0] != "@"]
SEMAPHORES = (["v", "a", "pe", "gi", "fac", "sx", "sy", "rp", "rd", "lay", "yd", "sent", "gf", "gd", "fa"]
              + ["wl%d" % d for d in WIN] + WRITES)


def unit(h):
    return 8 << (7 - h)


def tile(nm):
    return (int(nm[1]),) + {"": (0, 32), "a": (0, 16), "b": (16, 32)}[nm[2:]]


def rank_program(g, core, T, topo):
    rank = T.rank_of(core)
    if rank is None:
        return
    S = T.sem
    V, A, SY, PE = g.vector, g.scalar, g.sync, g.tensor
    op = AluOpType
    ACT = ActivationFunctionType
    W = [T.w0, T.w1]
    handed = [h for h in range(1, 7) if O[h] != O[h - 1]]

    def peer(d):
        return T.cores[(rank + d) % N]

    def reach(nm):
        h = int(nm[1] if nm[0] == "G" else nm[2])
        if nm[:2] == "ix":
            return h - (O[h - 1] if h in EARLY else O[h])
        return O[h + 1] - O[h] if nm[:2] in ("st", "sq") else -h

    nv, na = [0, 0], [0, 0]

    def issue(Q, sem, n, fn, after):
        if after > n[1]:
            Q.wait_ge(sem, after)
            n[1] = after
        fn().then_inc(sem, 1)
        n[0] += 1
        return n[0]

    def vec(fn, after=0):
        return issue(V, S.v, nv, fn, after)

    def act(fn, after=0):
        return issue(A, S.a, na, fn, after)

    ts = V.tensor_scalar

    first = {"fac": (T.fown[:], T.fac[:], S.fac),
             "sx": (T.stage[0], T.lay[14::16, :], S.sx), "sy": (T.stage[1], T.lay[15::16, :], S.sy),
             "px": (T.raw[:, 0:32], T.px[:], S.rp), "py": (T.raw[:, 32:64], T.py[:], S.rp),
             "dx": (T.raw[:, 64:96], T.dx[:], S.rd), "dy": (T.raw[:, 96:128], T.dy[:], S.rd),
             "pre": (T.w0[:, 0:PRE], T.lay[:, 0:PRE], S.wl0)}
    for Q, names in ((SY, SY_HEAD), (A, ACT_HEAD)):
        for nm in names:
            Q.dma_start(first[nm][0], first[nm][1]).then_inc(first[nm][2], 16)
    nlay = [0]

    def load_lay(n):
        for _ in range(n):
            k = nlay[0]
            SY.dma_start(T.ly[k::8, :], T.lay[k::8, :]).then_inc(S.lay, 16)
            nlay[0] += 1

    place = {nm: (j, len(c.split("+"))) for c in G_ORDER for j, nm in enumerate(c.split("+"))}

    def deal(src, dst, nm):
        j, n = place[nm]
        en = topo.engines(src, dst)
        cuts = {1: [0, 4], 2: [0, 2, 4], 3: [0, 1, 2, 4], 4: [0, 1, 2, 3, 4]}[n]
        return en[cuts[j] * len(en) // 4:cuts[j + 1] * len(en) // 4]

    def landed(Q, nm):
        Q.wait_ge(S[nm], len(deal(peer(-reach(nm)), core, nm)))

    sent = [0]

    def put(parts):
        trs = []
        for nm, out, in_ in parts:
            dst = peer(reach(nm))
            en = deal(core, dst, nm)
            rid, pid, _ = topo.addr(dst)
            sent[0] += len(en)
            if len(parts) == 1:
                g.remote_dma(out, in_, S[nm], S.sent, pid, rid, topo.mask(core, dst))
                return
            trs.append(RemoteDMATransfer(dst_ids=[DstId(rid=rid, pnc=pid)], dma_engine_mask=sum(1 << e for e in en),
                                         remote_sem=S[nm], srcs=[in_], dsts=[out]))
        g.remote_dma_fused(trs, local_sem=S.sent)

    def factors():
        g.wait_ge(S.fac, 16)
        m0 = topo.mask(core, peer(-IMPORTS[0]))
        ids = [topo.addr(peer(-d)) for d in IMPORTS]
        g.remote_dma_fused([RemoteDMATransfer(dst_ids=[DstId(rid=i[0], pnc=i[1]) for i in ids], dma_engine_mask=m0,
                                              remote_sem=S.fa, srcs=[T.fown[:]],
                                              dsts=[T.fl[:, d:d + 1] for d in IMPORTS])], local_sem=S.sent)
        sent[0] += len(topo.engines(core, peer(-IMPORTS[0])))

    nfa = sum(len(topo.engines(peer(d), peer(d - IMPORTS[0]))) for d in IMPORTS)

    wa, nA, wg = FILL0
    g.iota(T.w0[:, C - wg:C], [[0, wg]], 0, 0, allow_small_or_imprecise_dtypes=True).then_inc(S.gf, 1)
    g.iota(T.pid[:, 0:1], [[1, 1]], 0, 17).then_inc(S.gi, 1)
    g.iota(T.pid[:, 1:2], [[1, 1]], 0, 16).then_inc(S.gi, 1)
    g.iota(T.pat[:], [[2, 3], [1, 2]], ROW0, 0).then_inc(S.gi, 1)

    va = C - wg - nA * wa
    f0 = vec(lambda: V.memset(T.w0[:, PRE:PRE + wa], 0.0))
    f1 = vec(lambda: V.memset(T.w0[:, PRE + wa:va], 0.0))
    A.wait_ge(S.v, f0)
    for a in range(va, C - wg, wa):
        fa0 = act(lambda: A.activation(T.w0[:, a:a + wa], T.w0[:, PRE:PRE + wa], ACT.Copy))
    for Q, row in ((SY, OWN), (A, OWN + 1)):
        Q.wait_ge(S.gf, 1)
        Q.wait_ge(S.a, fa0)
        Q.wait_ge(S.v, f1)
        Q.dma_start(T.w0[row::16, PRE:], T.lay[row::16, PRE:]).then_inc(S.wl0, 16)
    na[1] = fa0
    loads = {d: 32 for d in IMPORTS}
    loads[0] = 48

    f2 = vec(lambda: V.memset(T.w1[:, 0:1024], 0.0))
    A.wait_ge(S.v, f2)
    for a in range(1024, FILL1[0], 512):
        b = min(a + 512, FILL1[0])
        act(lambda: A.activation(T.w1[:, a:b], T.w1[:, 0:b - a], ACT.Copy))

    V.wait_ge(S.gi, 3)
    vec(lambda: ts(T.k0[:, 0:1], T.pid[:, 0:1], 4, 1, op.arith_shift_right, op.bitwise_and))
    n = vec(lambda: ts(T.k0[:, 1:2], T.pid[:, 1:2], 255, None, op.bitwise_and))
    for a, b in ((0, 16), (272, 304), (560, 576)):
        vec(lambda: V.memset(T.gt[:, a:b], 0.0))
    vec(lambda: ts(T.k1[:, 0:1], T.k0[:, 0:1], 272.0, None, op.mult), n)
    n = vec(lambda: V.tensor_copy(T.k1[:, 1:2], T.k0[:, 1:2]))
    V.wait_ge(S.fac, 16)

    def factor(h):
        d = (h - O[h]) % N
        return vec(lambda: ts(T.fs[:, h:h + 1], T.fl[:, d:d + 1] if d else T.fown[:], unit(h + 1) / 128.0, None,
                              op.mult))

    factor(0)
    V.wait_ge(S.rp, 32)
    quarters = [(32 * u + 16 * s, 32 * s + 16 * u) for u in range(2) for s in range(2)]
    for a, b in quarters:
        p0 = vec(lambda: ts(T.hist[:, a:a + 16], T.raw[:, b:b + 16], float(unit(0)), None, op.mult))
    vec(lambda: ts(T.pick[:, 0:6], T.pat[:], T.k1[:, 0:1], T.k1[:, 1:2], op.add, op.add), n)

    def slot(k, a=0, b=64):
        return T.hist[:, 64 * k + a:64 * k + b]

    def lst(buf, j, a=0, b=32):
        return buf[:, 32 * j + a:32 * j + b]

    ready = {"sx": [(S.sx, 16)], "sy": [(S.sy, 16)]}

    def fields(k, h, u, after):
        vec(lambda: ts(T.cx[:, 16 * u:16 * u + 16], slot(k, 32 * u, 32 * u + 16), 14 - h, 127,
                       op.arith_shift_right, op.bitwise_and), after)
        return vec(lambda: ts(T.cy[:, 16 * u:16 * u + 16], slot(k, 32 * u + 16, 32 * u + 32), 7 - h, 63 * 128,
                              op.arith_shift_right, op.bitwise_and))

    def ahead(k, u):
        vec(lambda: V.tensor_tensor(T.pre[:, 32 * u:32 * u + 32], slot(k, 32 * u, 32 * u + 32),
                                    slot(k - 1, 32 * u, 32 * u + 32), op.subtract))

    def behind(k, h):
        n = vec(lambda: ts(slot(k + 1), slot(k), 0.25, BIAS * unit(h + 2) / 8, op.mult, op.add))
        ready["sq%d" % h] = [(S.v, n)]

    def cells(k, h, j, after, stepping=True):
        def join(u, n):
            return vec(lambda: V.tensor_tensor(lst(T.ixl, j, 16 * u, 16 * u + 16), T.cx[:, 16 * u:16 * u + 16],
                                               T.cy[:, 16 * u:16 * u + 16], op.add), n)
        n0 = fields(k, h, 0, after[0])
        if stepping:
            ahead(k, 0)
        n1 = fields(k, h, 1, after[1])
        m0 = join(0, n0)
        if stepping:
            ahead(k, 1)
            if h < 6:
                behind(k, h)
        return m0, join(1, n1)

    V.wait_ge(S.rd, 32)
    for a, b in quarters:
        n = vec(lambda: V.tensor_tensor(T.tw[:, a:a + 16], T.raw[:, b:b + 16], T.raw[:, 64 + b:80 + b], op.add))
    halves = {0: cells(0, 0, 0, (p0, p0), False)}
    made = {0: halves[0][1]}
    vec(lambda: ts(T.pre[:], T.tw[:], float(unit(1)), -BIAS * unit(1) / 8, op.mult, op.add), n)

    seen = set()

    def once(Q, key, fn):
        if (Q is V, key) not in seen:
            seen.add((Q is V, key))
            fn()

    def gather(Q, nm, a, b):
        h = int(nm[1])
        once(Q, "lay", lambda: Q.wait_ge(S.lay, 128))
        if O[h] == h:
            if Q is A:
                A.wait_ge(S.v, made[h])
            src = T.ly[:].indirect(lst(T.ixl, h, a, b))
        else:
            once(Q, h, lambda: landed(Q, "ix%d" % h))
            src = T.ly[:].indirect(lst(T.ixr, h, a, b))
        out = T.gs[:, 512 * h + 16 * a:512 * h + 16 * b]
        if Q is A:
            done = (S.a, act(lambda: A.activation(out, src, ACT.Copy)))
        else:
            done = (S.v, vec(lambda: V.tensor_copy(out, src), made.get(h, 0)))
        ready.setdefault(nm, []).append(done)

    cur = 0
    hops = {}
    gate = {}
    c = 16 * SPLIT
    for h in range(7):
        d = (h - O[h]) % N
        w, rho, _ = WIN[d]
        if h in handed:
            if "sq%d" % (h - 1) in WRITES:
                landed(V, "sq%d" % (h - 1))
            landed(V, "st%d" % (h - 1))
            cur += 2
            halves[h] = cells(cur, h, h, (last, last))
            made[h] = halves[h][1]
            if h not in EARLY:
                ready["ix%d" % h] = [(S.v, made[h])]
        for Q in (V, A):
            for dd, (w2, _, gt) in WIN.items():
                if w2 == w and (gt is None or gt < h):
                    once(Q, "w%d" % dd, lambda: Q.wait_ge(S["wl%d" % dd], loads[dd]))
        fsc, rb = T.fs[:, h:h + 1], RB * unit(h + 1) / 8
        gv, ga, turned, picked = {}, {}, {}, {}
        for u in range(2):
            a = 288 * u + 16
            gv[u] = vec(lambda: ts(T.gt[:, a:a + c], W[w][:].indirect(lst(T.ixl, h, 16 * u, 16 * u + SPLIT)), fsc, rb,
                                   op.mult, op.add), halves[h][u])
            A.wait_ge(S.v, halves[h][u])
            ga[u] = act(lambda: A.activation(T.gt[:, a + c:a + 256],
                                             W[w][:].indirect(lst(T.ixl, h, 16 * u + SPLIT, 16 * u + 16)),
                                             ACT.Identity, bias=rb, scale=fsc))
        gate[h] = (gv[1], ga[1])
        for u in range(2):
            V.wait_ge(S.a, ga[u])
            vec(lambda: V.transpose(T.tt[:, 544 * u + 256:544 * u + 544], T.gt[:, 288 * u:288 * u + 288]), gv[u])
            turned[u] = vec(lambda: V.transpose(T.tt[:, 544 * u:544 * u + 256], T.gt[:, 288 * u + 16:288 * u + 272]))
        i = (rho - ROW0) // 2
        for u in range(2):
            picked[u] = vec(lambda: V.tensor_tensor(
                slot(cur + 2, 32 * u, 32 * u + 32), T.tt[:, 544 * u:544 * u + 544].indirect(T.pick[:, 2 * i:2 * i + 2]),
                T.pre[:, 32 * u:32 * u + 32], op.add), turned[u])
            if u == 0 and h == 0:
                behind(0, 0)
            elif u == 0 and h < 6:
                factor(h + 1)
                if h in IDENT_IN:
                    a = 64 * IDENT_IN.index(h)
                    once(V, "id", lambda: V.wait_ge(S.gd, 1))
                    idn = vec(lambda: ts(T.ident[:, a:a + 64], T.dif[:, a:a + 64], 0.0, None, op.is_equal))
        last = picked[1]
        cur += 2
        if h + 1 in handed:
            ready["st%d" % h] = [(S.v, last)]
            hops[h] = cur
            if h + 1 in EARLY:
                last = cells(cur, h + 1, 8, picked, False)[1]
                ready["ix%d" % (h + 1)] = [(S.v, last)]
        else:
            halves[h + 1] = cells(cur, h + 1, h + 1, picked, h < 6)
            made[h + 1] = halves[h + 1][1]
            ready["ix%d" % (h + 1)] = [(S.v, made[h + 1])]
        if h == 0:
            f3 = vec(lambda: V.memset(T.w1[:, FILL1[1]:FILL1[2]], 0.0))
            for a in range(FILL1[0], FILL1[1], 1024):
                b = min(a + 1024, FILL1[1])
                fa1 = act(lambda: A.activation(T.w1[:, a:b], T.w1[:, 0:b - a], ACT.Copy))
            V.wait_ge(S.fa, nfa)
            last = factor(1)
        for e, a, b in ACT_E.get(h, []):
            gather(A, "G%d" % e, a, b)
        for e, a, b in DVE_E.get(h, []):
            gather(V, "G%d" % e, a, b)
    for q, nm, a, b in LAST:
        gather(V if q == "V" else A, nm, a, b)

    def reload(d):
        w, rho, gt = WIN[d]
        if gt is None:
            SY.wait_ge(S.gf, 1 + G_ORDER.count("fill"))
            SY.wait_ge(S.a, fa1)
            SY.wait_ge(S.v, f3)
        else:
            SY.wait_ge(S.v, gate[gt][0])
            SY.wait_ge(S.a, gate[gt][1])
        for s, nm in enumerate(("sx%d" % d, "sy%d" % d)):
            landed(SY, nm)
            if s == 1 and "st%s" % gt in ready:
                SY.wait_ge(*ready["st%d" % gt][0])
            SY.dma_start(W[w][rho + s::16, :], T.land[2 * IMPORTS.index(d) + s]).then_inc(S["wl%d" % d], 16)

    for what, x in SYNC_ORDER:
        if what == "lay":
            load_lay(x)
        elif what == "win":
            reload(x)
        elif what == "gate":
            SY.wait_ge(S.v, gate[x][0])
        elif x == "wl0":
            SY.wait_ge(S.wl0, loads[0])
        else:
            landed(SY, x)

    for name in G_ORDER:
        if name == "id":
            g.iota(T.dif[:], [[1, 128]], 0, -1).then_inc(S.gd, 1)
            continue
        if name == "fa":
            factors()
            continue
        if name[0] == "@":
            landed(g, name[1:])
            continue
        if name == "fill":
            g.iota(T.w1[:, FILL1[2]:C], [[0, C - FILL1[2]]], 0, 0,
                   allow_small_or_imprecise_dtypes=True).then_inc(S.gf, 1)
            continue
        parts = []
        for nm in name.split("+"):
            kind = nm[:2]
            for s, n in ready[kind if kind in ("sx", "sy") else nm]:
                g.wait_ge(s, n)
            if nm[0] == "G":
                h, a, b = tile(nm)
                a, b = 512 * h + 16 * a, 512 * h + 16 * b
                parts.append((nm, T.gl[:, a:b], T.gs[:, a:b]))
                continue
            h = int(nm[2])
            if kind in ("sx", "sy"):
                s = int(kind == "sy")
                parts.append((nm, T.land[2 * IMPORTS.index(h) + s], T.stage[s]))
            elif kind == "st":
                a = -64 * ("sq%d" % h not in WRITES)
                parts.append((nm, slot(hops[h] + 2, a), slot(hops[h], a)))
            elif kind == "sq":
                parts.append((nm, slot(hops[h] + 1), slot(hops[h] - 1)))
            else:
                parts.append((nm, lst(T.ixr, h), lst(T.ixl, 8 if h in EARLY else h)))
        put(parts)
    g.wait_ge(S.sent, sent[0])

    wy = 512 // STORES
    PE.wait_ge(S.v, idn)
    for j, h in enumerate(PE_ORDER):
        if h == 0:
            for s, n in ready["G0"]:
                PE.wait_ge(s, n)
            src = T.gs
        else:
            landed(PE, "G%d" % h)
            src = T.gl
        for u in range(STORES):
            a = 512 * h + wy * u
            mm = PE.matmul(T.ps[:, 512 * u:512 * u + wy], T.ident[:], src[:, a:a + wy], j == 0, j == 6)
            if j == 6:
                mm.then_inc(S.pe, 1)
    for u in range(STORES):
        nm = FINAL[2 * u // STORES]
        h, a, b = int(nm[1]), wy * u, wy * u + wy
        V.wait_ge(S.pe, u + 1)
        landed(V, nm)
        n = vec(lambda: V.tensor_tensor(T.ys[:, a:b], T.ps[:, 512 * u:512 * u + wy],
                                        T.gl[:, 512 * h + a:512 * h + b], op.add))
        Q = (SY, A)[u % 2]
        Q.wait_ge(S.v, n)
        Q.dma_start(T.y[:, a:b], T.ys[:, a:b]).then_inc(S.yd, 16)
    SY.wait_ge(S.yd, 16 * STORES)
